import numpy as np, ml_dtypes
CORES = [3,7,11,15,131,135,139,143]
N = 8
import mx_ref
BF = ml_dtypes.bfloat16
def gentries(a):
    return np.ascontiguousarray(a.reshape(8, 16, -1).transpose(0, 2, 1)).reshape(8, -1)
def gtable(e):
    e = np.asarray(e); return np.ascontiguousarray(e.reshape(8, -1, 16).transpose(0, 2, 1)).reshape(128, -1).astype(np.int32)
def gcols(t, e):
    v = np.concatenate([t.reshape(8, 16, -1, 4), np.zeros((8, 16, 1, 4), BF)], axis=2)
    return np.ascontiguousarray(np.stack([v[g][:, e[g]] for g in range(8)])).reshape(128, -1)
def gpick(z, e):
    return np.concatenate([z[16 * g:16 * g + 16][:, e[g]] for g in range(8)])
def pick(q, e):
    c = np.concatenate([q[0].reshape(128, -1, 4), np.zeros((128, 1, 4), np.uint8)], axis=1); s = np.concatenate([q[1], np.ones((16, 1), np.uint8)], axis=1)
    return (np.ascontiguousarray(c[:, e].reshape(128, -1)), np.ascontiguousarray(s[:, e]))
def join(*qs):
    return (np.concatenate([q[0] for q in qs], axis=1), np.concatenate([q[1] for q in qs], axis=1))
def put(q, e, v):
    c, s = q[0].reshape(128, -1, 4).copy(), q[1].copy(); c[:, e] = v[0].reshape(128, -1, 4); s[:, e] = v[1]
    return (c.reshape(128, -1), s)
def pk(c, s):
    return (np.ascontiguousarray(c), mx_ref.live(s))
def emit(q):
    return q[0], q[1]
def packed(v, rng):
    q = [mx_ref.quantize(np.ascontiguousarray(v[r])) for r in range(N)]
    return np.stack([a for a, b in q]), np.stack([mx_ref.plane(b, rng) for a, b in q])
def values_of_codes():
    e, c = np.zeros((128, 128, 4), np.float32), np.zeros((128, 2, 4), np.uint8)
    e[np.arange(128), np.arange(128), 0] = 1
    c[:127, :, 0] = np.arange(256).reshape(2, 128).T[:127]
    return mx_ref.matmul(mx_ref.quantize(e.reshape(128, 512).astype(BF)), (c.reshape(128, 8), np.full((16, 2), 127, np.uint8))).T.reshape(-1).astype(np.float64)
CODE_VALUE, SCALE_VALUE = values_of_codes(), 2.0 ** (np.arange(256) - 127.0)
def decode(q):
    return (CODE_VALUE[q[0]].reshape(16, 8, -1, 4) * SCALE_VALUE[q[1]][:, None, :, None] + 0.0).reshape(128, -1).astype(np.float32)
def f(rng, *shape):
    return mx_ref.flush((rng.standard_normal(shape, dtype=np.float32) * np.exp2(rng.integers(-2, 3, shape[:-1] + (1,)))).astype(BF))
def wide(rng, *shape, cols=0):
    v = rng.standard_normal(shape, dtype=np.float32) * np.exp2(rng.integers(-12, 13, shape)).astype(np.float32)
    if cols: v *= np.repeat(np.exp2(rng.integers(-cols, cols + 1, shape[:-2] + (1, shape[-1] // 4))) * (rng.random(shape[:-2] + (1, shape[-1] // 4)) > 0.0625), 4, axis=-1).astype(np.float32)
    return mx_ref.flush(v.astype(BF))
V, F, K, T = 384, 768, 96, 3
def big(v, k):
    v = v.astype(np.float32) * np.float32(k)
    v[np.abs(v) < np.float32(2.0 ** -16)] = 0
    return v.astype(BF)
def weights(rng, k=1.0, still=slice(0)):
    v = big(f(rng, N, 128, 2048), k).reshape(N, 128, 4, 128, 4)
    v[:, :, :, still] = 0
    c, s = packed(v.reshape(N, 128, 2048), rng)
    return {"wc": c, "ws": s}
def lists_of(rng):
    return rng.permuted(np.tile(np.arange(F) % V, (N, 8, 1)), axis=2)
def stored(e):
    return np.stack([gtable(e[r]) for r in range(N)])
def numbers_of(rng):
    return {"x": big(f(rng, N, 128, 4 * V), 1), "fv": stored(lists_of(rng)), "u": np.array(f(rng, N, 128, 512)), "wy": np.array(f(rng, N, 128, 512))}
def planted(rng):
    at = 16 * rng.permutation(8)[:T]
    still = np.concatenate([np.arange(p, p + 16) for p in at])
    d = numbers_of(rng)
    x = d["x"].reshape(N, 128, V, 4)
    x[:, still] = 0
    d["u"][:, :, :4 * T] = 0
    d["u"][:, at, 4 * np.arange(T)] = 1
    return {**d, **weights(rng, 1.0, still)}, x, at
def setup_inputs(rng):
    return {**numbers_of(rng), **weights(rng)}
def setup_inputs_ties(rng):
    d, x, at = planted(rng)
    o = rng.permutation(N)
    none = int(rng.integers(T))
    for i in range(N):
        zero = i < N // 2
        for t in range(T):
            v = np.full(V, 0.0 if zero else 1.0, np.float32)
            j = rng.permutation(V)
            v[j[:K // 4]] = 2
            if zero: v[j[K // 4:K // 2]] = -2
            if i == 0: v *= np.float32(2.0 ** -24)
            if i == 0 and t == none: v[:] = 0
            if i == N - 1: v *= np.float32(2.0 ** 26)
            x[o[i], at[t], :, 0] = v.astype(BF)
    d["u"][o[0], at, 4 * np.arange(T)] = 2.0 ** -30
    d["u"][o[N - 1], at, 4 * np.arange(T)] = 2.0 ** 30
    return {**d, "x": x.reshape(N, 128, 4 * V)}
def setup_inputs_near(rng):
    d, x, at = planted(rng)
    e = lists_of(rng)
    sign = (rng.permutation(N) % 2 * 2.0 - 1.0).astype(np.float32).astype(BF)
    for t in range(T):
        p = int(at[t])
        e[:, p // 16] = np.arange(F) // 2
        d["u"][:, p + 1, 4 * t] = 2.0 ** 12
        d["u"][:, p + 8:p + 11, 4 * t:4 * t + 4] = 1
        x[:, p, :, 0] = sign[:, None]
        for r in range(N):
            s = np.argsort(np.argsort(np.arange(V) + 16 * rng.random(V)))
            s = (s + int(rng.integers(1, V // 4))) % V
            v = (((s[:, None] >> np.arange(12)) & 1) * np.exp2(np.arange(12) - 23.0)).astype(np.float32).astype(BF)
            x[r, p + 8:p + 11] = v.reshape(V, 3, 4).transpose(1, 0, 2)
            j = rng.permutation(V)[:8]
            x[r, p + 1, j[:4], 0] = 2.0 ** 30
            x[r, p + 1, j[4:], 0] = -2.0 ** 30
    m = int(rng.integers(N))
    later = [int(p) for p in at[1:]]
    d["u"][m, :, :4] = 0
    for p in range(0, 128, 16):
        if p in later: continue
        d["u"][m, p, 0] = 1
        d["u"][m, p + 8:p + 16, 0] = 1
        v = rng.integers(8, 16, (16, V, 4)) * rng.choice([-1.0, 1.0], (16, V, 4))
        v[:8] *= 2.0 ** -3
        v[8:] *= 2.0 ** -27
        v[0, :, 0] = 1
        x[m, p:p + 16] = v.astype(np.float32).astype(BF)
    return {**d, "x": x.reshape(N, 128, 4 * V), "fv": stored(e)}
def setup_inputs_deep(rng):
    d = numbers_of(rng)
    e = lists_of(rng)
    line = 1.0 - 2.0 * rng.integers(0, 2, (128, 4))
    sign = np.tile((rng.permutation(N) % 2 * 2.0 - 1.0)[:, None], (1, V))
    m = int(rng.permutation(np.flatnonzero(sign[:, 0] > 0))[0])
    j, k = rng.permutation(V), rng.permutation(F)
    sign[m, j[K // 4:]] = -1
    e[m][:, k[:K // 2]] = rng.permuted(np.tile(j[:K // 4], (8, 2)), axis=1)
    e[m][:, k[K // 2:]] = rng.permuted(np.tile(j[K // 4:], (8, 2)), axis=1)
    d["u"][:, :, :4 * T] = (np.tile(line, (1, T)) * 2.0 ** 30).astype(np.float32).astype(BF)
    x = np.where(rng.random((N, 128, V, 4)) < 0.0625, 0.875, 1.0) * 2.0 ** 30
    x = x * line[:, None, :] * sign[:, None, :, None]
    return {**d, "x": x.astype(np.float32).astype(BF).reshape(N, 128, 4 * V), "fv": stored(e), **weights(rng, 2.0 ** -5)}
def setup_inputs_crowd(rng):
    d, x, at = planted(rng)
    e = np.zeros((N, 8, F), int)
    for r in range(N):
        odd = bin(r).count("1") % 2
        turn = int(rng.integers(T))
        to = rng.permuted(np.tile(np.arange(V), (8, 1)), axis=1)
        e[r] = to[:, np.arange(F) % V if odd else np.arange(F) // 2]
        for t in range(T):
            v = np.ones(V, np.float32)
            if odd:
                j = 2 * rng.permutation(V // 2)[:K // 2] + rng.integers(0, 2, K // 2)
                if t == turn: j = 8 * rng.permutation(V // 8)[:K // 2] + int(rng.integers(8))
                v[j] = 64 * (1 + 0.25 * rng.integers(0, 4, K // 2))
            else:
                j = rng.permutation(V // 2)[:K // 4]
                up = rng.permutation(K // 4) % 2
                v[j + V // 2 * up] = 1024 * (1 + 0.25 * rng.integers(0, 4, K // 4))
                v[j + V // 2 * (1 - up)] = 64 * (1 + 0.25 * rng.integers(0, 4, K // 4))
            p = int(at[t])
            x[r, p, to[p // 16], 0] = v.astype(BF)
    return {**d, "x": x.reshape(N, 128, 4 * V), "fv": stored(e)}
def setup_inputs_spread(rng):
    d = setup_inputs(rng)
    d["x"] = big(wide(rng, N, 128, 4 * V, cols=6), 1)
    return d
def check_inputs(d):
    b = []
    for k in ("x", "u", "wy"):
        v = np.abs(d[k].astype(np.float32))
        if not (np.isfinite(v).all() and ((v == 0) | (v >= 2.0 ** -30) & (v <= 2.0 ** 30)).all()): b.append("a value of " + k)
    e = [gentries(a) for a in d["fv"]]
    if any(((a < 0) | (a >= V)).any() for a in e): b.append("an entry of fv out of range")
    if any((np.sort(a, axis=1) != np.arange(F) // 2).any() for a in e): b.append("a variable that isn't exactly twice in a list of fv")
    good = True
    for r in range(N):
        try:
            w = decode(pk(d["wc"][r], d["ws"][r]))
            good = good and bool(np.isfinite(w).all() and (np.abs(w) <= 2.0 ** 31).all())
        except Exception:
            good = False
    if not good: b.append("a number that wc and ws hold")
    return b
def reference(x, fv, u, wy, wc, ws):
    now = [x[r] for r in range(N)]
    e = [gentries(fv[r]) for r in range(N)]
    qu = [mx_ref.quantize(np.ascontiguousarray(u[r])) for r in range(N)]
    qw = [pk(wc[r], ws[r]) for r in range(N)]
    fl = np.zeros((N, T, K), np.float32)
    for t in range(T):
        fired, sent = [], []
        for r in range(N):
            h = mx_ref.quantize(gcols(now[r], e[r]))
            s = mx_ref.matmul(qu[r], h)[t] + np.float32(0.0)
            o = np.argsort(-s, kind="stable")[:K]
            fired.append(o)
            sent.append(pick(h, o))
            fl[r, t] = o
        new = []
        for r in range(N):
            p = r ^ (1 << t)
            low = np.full((8, V), K)
            np.minimum.at(low, (np.arange(8)[:, None], e[r][:, fired[p]]), np.tile(np.arange(K), (8, 1)))
            v = []
            for b in range(4):
                z = mx_ref.matmul(pick(qw[r], np.arange(128 * b, 128 * b + 128)), sent[p]) * np.float32(0.03125)
                v.append(gpick(np.concatenate([z, np.zeros((128, 1), np.float32)], axis=1), low))
            v = np.stack(v, axis=2).reshape(128, -1)
            hit = np.repeat(np.repeat(low < K, 16, axis=0), 4, axis=1)
            a = now[r].astype(np.float32)
            new.append(np.where(hit, a * np.float32(0.5) + v * np.float32(0.5), a).astype(BF))
        now = new
    y = np.zeros((N, 128, V), np.float32)
    oc, osc = np.zeros((N, 128, 4 * V), np.uint8), np.zeros((N, 16, V), np.uint8)
    for r in range(N):
        q = mx_ref.quantize(np.ascontiguousarray(now[r]))
        y[r] = mx_ref.matmul(mx_ref.quantize(np.ascontiguousarray(wy[r])), q)
        oc[r], osc[r] = emit(q)
    return {"y": y, "oc": oc, "osc": osc, "fl": fl}

@@ -1,0 +1,439 @@
+from concourse.mybir import dt, AluOpType, ActivationFunctionType
+
+ALU = AluOpType
+ACT = ActivationFunctionType
+V, F, K, ROUNDS = 384, 768, 96, 3
+SPARE = 512
+CODE = "float8_e4m3fn_x4"
+
+SCRATCH = {
+    "ps": ("psum", [128, 4096], "float32"),
+    "fvi": ("sbuf", [128, 48], "int32"),
+    "fvu": ("sbuf", [128, 48], "uint16"),
+    "o4": ("sbuf", [128, 192], "uint16"),
+    "xs": ("sbuf", [128, 4 * (SPARE + V)], "bfloat16"),
+    "hs": ("sbuf", [128, 4 * F], "bfloat16"),
+    "ub": ("sbuf", [128, 512], "bfloat16"),
+    "qu": ("sbuf", [128, 128], CODE),
+    "su": ("sbuf", [128, 128], "uint8"),
+    "ubc": ("sbuf", [128, 384], CODE),
+    "sbc": ("sbuf", [128, 384], "uint8"),
+    "uoff": ("sbuf", [128, 24], "uint16"),
+    "wyb": ("sbuf", [128, 512], "bfloat16"),
+    "qwy": ("sbuf", [128, 128], CODE),
+    "swy": ("sbuf", [128, 128], "uint8"),
+    "qw": ("sbuf", [128, 512], CODE),
+    "sw": ("sbuf", [128, 512], "uint8"),
+    "qx": ("sbuf", [128, V], CODE),
+    "sx": ("sbuf", [128, V], "uint8"),
+    "ysb": ("sbuf", [128, V], "float32"),
+    "scol": ("sbuf", [128, 8], "float32"),
+    "acc": ("sbuf", [128, 8], "float32"),
+    "flags": ("sbuf", [128, 3328], "bfloat16"),
+    "sg": ("sbuf", [128, 2304], "bfloat16"),
+    "cnt": ("sbuf", [128, 2304], "float16"),
+    "tot": ("sbuf", [128, 8], "float32"),
+    "pos": ("sbuf", [128, 8], "uint16"),
+    "pw": ("sbuf", [128, F], "float32"),
+    "p2": ("sbuf", [128, 192], "float32"),
+    "tr": ("sbuf", [128, 192], "float32"),
+    "u1": ("sbuf", [128, 8], "float32"),
+    "u2": ("sbuf", [128, 8], "float32"),
+    "u3": ("sbuf", [128, 8], "float32"),
+    "num": ("sbuf", [128, F], "float32"),
+    "fvrow": ("sbuf", [128, F], "float32"),
+    "pidx": ("sbuf", [128, 4], "int32"),
+    "pcol": ("sbuf", [128, 4], "float32"),
+    "fid": ("sbuf", [128, K], "float32"),
+    "dif": ("sbuf", [128, K], "float32"),
+    "m1": ("sbuf", [128, K], "float32"),
+    "m2": ("sbuf", [128, K], "float32"),
+    "msk": ("sbuf", [128, K], "float32"),
+    "rmin": ("sbuf", [128, K], "float32"),
+    "rst": ("sbuf", [128, 6 * K], "bfloat16"),
+    "dupi": ("sbuf", [128, 12], "float32"),
+    "dup": ("sbuf", [128, 12], "uint16"),
+    "f4": ("sbuf", [128, 24], "uint16"),
+    "ob": ("sbuf", [128, 24], "uint16"),
+    "gt": ("sbuf", [128, K], "float32"),
+    "gu": ("sbuf", [128, K], "float32"),
+    "s1": ("sbuf", [128, K], "float32"),
+    "eq": ("sbuf", [128, 6 * K], "bfloat16"),
+    "los": ("sbuf", [128, 6 * K], "bfloat16"),
+    "dst": ("sbuf", [128, 8], "float32"),
+    "x32": ("sbuf", [128, 4 * K], "float32"),
+    "sm": ("sbuf", [128, 4 * K], "float32"),
+    "zb": ("sbuf", [128, 4 * K], "bfloat16"),
+}
+for _t in range(ROUNDS):
+    SCRATCH["qh%d" % _t] = ("sbuf", [128, F], CODE)
+    SCRATCH["sh%d" % _t] = ("sbuf", [128, F], "uint8")
+    SCRATCH["fo%d" % _t] = ("sbuf", [128, 6], "uint16")
+    SCRATCH["lst%d" % _t] = ("sbuf", [128, 6], "uint16")
+    SCRATCH["slotq%d" % _t] = ("sbuf", [128, K], CODE)
+    SCRATCH["slots%d" % _t] = ("sbuf", [128, K], "uint8")
+    SCRATCH["landq%d" % _t] = ("sbuf", [128, K + 128], CODE)
+    SCRATCH["lands%d" % _t] = ("sbuf", [128, K + 128], "uint8")
+    SCRATCH["flr%d" % _t] = ("sbuf", [128, K], "float32")
+
+SEMAPHORES = ["cv", "cs", "cp", "cg", "sent", "dfv", "dx", "du", "dwc", "dws", "dwy", "dout", "dy"]
+SEMAPHORES += ["list%d" % _t for _t in range(ROUNDS)] + ["data%d" % _t for _t in range(ROUNDS)]
+SEMAPHORES += ["dfl%d" % _t for _t in range(ROUNDS)]
+
+
+def _overlap(a, b):
+    if a[0] != b[0]:
+        return False
+    if a[0] == "ps":
+        ba = set(c // 512 for c in range(a[3], a[4], a[5]))
+        bb = set(c // 512 for c in range(b[3], b[4], b[5]))
+        return bool(ba & bb)
+    if a[2] <= b[1] or b[2] <= a[1] or a[4] <= b[3] or b[4] <= a[3]:
+        return False
+    if a[5] == b[5] and a[5] > 1 and a[3] % a[5] != b[3] % b[5]:
+        return False
+    return True
+
+
+def _mask(engines):
+    m = 0
+    for e in engines:
+        m |= 1 << e
+    return m
+
+
+def rank_program(g, core, T, topo):
+    rank = T.rank_of(core)
+    if rank is None:
+        return
+    partners = [T.cores[rank ^ (1 << t)] for t in range(ROUNDS)]
+
+    def lanes(src):
+        r = T.rank_of(src)
+        eng = [topo.engines(src, T.cores[r ^ (1 << t)]) for t in range(ROUNDS)]
+        common = [e for e in eng[0] if all(e in x for x in eng)]
+        out = []
+        for x in eng:
+            more = [e for e in x if e not in common]
+            out.append((common, more if len(more) == len(common) else common))
+        return out
+
+    mine = lanes(core)
+    theirs = [lanes(partners[t])[t] for t in range(ROUNDS)]
+
+    eng = {"v": g.vector, "s": g.scalar, "p": g.tensor, "g": g, "y": g.sync}
+    own = {"v": "cv", "s": "cs", "p": "cp", "g": "cg"}
+    total = {}
+    known = {q: {} for q in eng}
+    log = []
+
+    def w(name, lo=None, hi=None, step=1, p0=0, p1=128):
+        t = T[name]
+        if lo is None:
+            lo, hi = 0, t.shape[1]
+        cols = slice(lo, hi) if step == 1 else slice(lo, hi, step)
+        ap = t[:, cols] if (p0, p1) == (0, 128) else t[p0:p1, cols]
+        return (ap, [(name, p0, p1, lo, hi, step)])
+
+    def words(a):
+        return (a[0].bitcast(dt.uint32), a[1])
+
+    def octets(a):
+        return (a[0].bitcast(dt.uint8), a[1])
+
+    def by(win, off):
+        return (win[0].indirect(off[0]), win[1] + off[1])
+
+    def wait(q, sem, count, clock):
+        k = known[q]
+        if k.get(sem, 0) < count:
+            eng[q].wait_ge(T.sem[sem], count)
+            k[sem] = count
+        for s, c in clock.items():
+            if k.get(s, 0) < c:
+                k[s] = c
+
+    def order(q, reads, writes):
+        need = {}
+        for (reg, wr, q0, sem, count, clock) in log:
+            hit = any(_overlap(reg, x) for x in writes)
+            if not hit and (wr or (reg[0] == "ps" and q0 != q)):
+                hit = any(_overlap(reg, x) for x in reads)
+            if hit and known[q].get(sem, 0) < count and need.get(sem, (0,))[0] < count:
+                need[sem] = (count, clock)
+        for sem in sorted(need, key=lambda s: -len(need[s][1])):
+            wait(q, sem, need[sem][0], need[sem][1])
+
+    def note(q, sem, inc, reads, writes):
+        total[sem] = total.get(sem, 0) + inc
+        clock = dict(known[q])
+        for r in reads:
+            log.append((r, False, q, sem, total[sem], clock))
+        for r in writes:
+            log.append((r, True, q, sem, total[sem], clock))
+
+    def op(q, call, out, ins, extra=None):
+        reads = [r for a in ins for r in a[1]]
+        writes = list(out[1][:1]) + (list(extra[1]) if extra else [])
+        reads += out[1][1:]
+        order(q, reads, writes)
+        call().then_inc(T.sem[own[q]], 1)
+        note(q, own[q], 1, reads, writes)
+
+    def dma(q, sem, out, in_):
+        order(q, in_[1], out[1])
+        eng[q].dma_start(out[0], in_[0]).then_inc(T.sem[sem], 16)
+        note(q, sem, 16, in_[1], out[1])
+
+    def hbm(ap):
+        return (ap, [])
+
+    def ts(out, a, s1, s2, op0, op1=None, q="v"):
+        ins = [a] + [s for s in (s1, s2) if isinstance(s, tuple)]
+        x1 = s1[0] if isinstance(s1, tuple) else s1
+        x2 = s2[0] if isinstance(s2, tuple) else s2
+        if op1 is None:
+            op(q, lambda: g.vector.tensor_scalar(out[0], a[0], x1, None, op0), out, ins)
+        else:
+            op(q, lambda: g.vector.tensor_scalar(out[0], a[0], x1, x2, op0, op1), out, ins)
+
+    def tt(out, a, b, o):
+        op("v", lambda: g.vector.tensor_tensor(out[0], a[0], b[0], o), out, [a, b])
+
+    def cp(out, a):
+        op("v", lambda: g.vector.tensor_copy(out[0], a[0]), out, [a])
+
+    def fill(out, c):
+        op("v", lambda: g.vector.memset(out[0], c), out, [])
+
+    def scan(out, a, b, init, op0, op1):
+        op("v", lambda: g.vector.tensor_tensor_scan(out[0], a[0], b[0], init, op0, op1), out, [a, b])
+
+    def quant(codes, scales, a):
+        op("v", lambda: g.vector.quantize_mx(codes[0], scales[0], a[0]), codes, [a], scales)
+
+    def act(out, a, func, bias=None, scale=None, accum=None):
+        kw = {}
+        ins = [a]
+        if bias is not None:
+            kw["bias"] = bias[0] if isinstance(bias, tuple) else bias
+            if isinstance(bias, tuple):
+                ins.append(bias)
+        if scale is not None:
+            kw["scale"] = scale
+        if accum is not None:
+            kw["accum_out"] = accum[0]
+        op("s", lambda: g.scalar.activation(out[0], a[0], func, **kw), out, ins, accum)
+
+    def mm(out, lq, ls, rq, rs):
+        op("p", lambda: g.tensor.matmul_mx(out[0], lq[0], ls[0], rq[0], rs[0], True, True), out, [lq, ls, rq, rs])
+
+    def iota(out, pattern, base, mult, small=True):
+        if small:
+            op("g", lambda: g.iota(out[0], pattern, base, mult, allow_small_or_imprecise_dtypes=True), out, [])
+        else:
+            op("g", lambda: g.iota(out[0], pattern, base, mult), out, [])
+
+    def remote(t, sem, dst, src, engines):
+        order("g", src[1], [])
+        rid, pid = topo.addr(partners[t], core)
+        g.remote_dma(dst[0], src[0], T.sem[sem], T.sem["sent"], pid, rid, _mask(engines))
+        total["sent"] = total.get("sent", 0) + len(engines)
+
+    for t in range(ROUNDS):
+        a, b = len(theirs[t][0]), len(theirs[t][1])
+        total["list%d" % t] = a
+        total["data%d" % t] = a + b
+        log.append((w("lst%d" % t)[1][0], True, "far", "list%d" % t, a, {}))
+        log.append((w("landq%d" % t, 0, K)[1][0], True, "far", "data%d" % t, a + b, {}))
+        log.append((w("lands%d" % t, 0, K)[1][0], True, "far", "data%d" % t, a + b, {}))
+
+    dma("y", "dfv", w("fvi"), hbm(T.fv[:]))
+    dma("s", "du", w("ub"), hbm(T.u[:]))
+    dma("y", "dx", w("xs", 0, 4 * V), hbm(T.x[:]))
+    wait("y", "dx", 16, {})
+    dma("y", "dwc", octets(w("qw")), hbm(T.wc[:]))
+    dma("y", "dws", w("sw"), hbm(T.ws[:]))
+    dma("y", "dwy", w("wyb"), hbm(T.wy[:]))
+
+    iota(w("pidx", 0, 1), [[0, 1]], 0, 1, small=False)
+    iota(w("fid"), [[128, 6], [1, 16]], 0, 0)
+    iota(w("dif"), [[0, 6], [1, 16]], 0, 0)
+    iota(w("dupi"), [[16, 6], [0, 2]], 0, 0)
+    iota(w("num"), [[1, F]], 0, 0)
+    for t in range(ROUNDS):
+        fill(w("uoff", 8 * t, 8 * t + 8), t)
+    fill(w("pw", 0, K), 0.0)
+    fill(w("rmin"), 0.0)
+    fill(w("rst"), 1.0)
+    fill(w("eq"), 0.0)
+    fill(w("rmin", 0, K, 16), 1.0e6)
+    fill(w("rst", 0, 6 * K, K), 0.0)
+    ts(w("pidx", 1, 2), w("pidx", 0, 1), 15, None, ALU.bitwise_and)
+    ts(w("pidx", 2, 3), w("pidx", 0, 1), 112, None, ALU.bitwise_and)
+    cp(w("pcol", 0, 2), w("pidx", 1, 3))
+    ts(w("fid"), w("fid"), w("pcol", 1, 2), None, ALU.add)
+    ts(w("dif"), w("dif"), w("pcol", 0, 1), None, ALU.subtract)
+    ts(w("dup"), w("dupi"), w("pcol", 0, 1), None, ALU.add)
+    ts(w("m1"), w("dif"), 0.0, 1.0 / SPARE, ALU.is_equal, ALU.mult)
+    ts(w("m2"), w("dif"), 0.0, 1024.0, ALU.is_gt, ALU.mult)
+    ts(w("msk"), w("dif"), 0.0, None, ALU.is_lt)
+    tt(w("m1"), w("m1"), w("m2"), ALU.add)
+    tt(w("msk"), w("msk"), w("m1"), ALU.add)
+    for e in range(4):
+        ts(w("o4", 48 * e, 48 * e + 48), w("fvi"), 4.0, float(e), ALU.mult, ALU.add)
+    quant(w("qu"), w("su"), w("ub"))
+
+    def spread_u(a, b):
+        off = w("uoff", 8 * a, 8 * b)
+        cp(words(w("ubc", 128 * a, 128 * b)), by(words(w("qu")), off))
+        act(w("sbc", 128 * a, 128 * b), by(w("su"), off), ACT.Copy)
+
+    spread_u(0, 1)
+
+    def bank(b, lo=0, hi=V):
+        return w("ps", 512 * b + lo, 512 * b + hi)
+
+    for t in range(ROUNDS):
+        qh, sh = "qh%d" % t, "sh%d" % t
+        uq, us = w("ubc", 128 * t, 128 * t + 128), w("sbc", 128 * t, 128 * t + 128)
+        for e in range(4):
+            src = by(w("xs", 0, 4 * V), w("o4", 48 * e, 48 * e + 48))
+            if e < 2:
+                cp(w("hs", e, 4 * F, 4), src)
+            else:
+                act(w("hs", e, 4 * F, 4), src, ACT.Copy)
+        for h in range(2):
+            quant(w(qh, V * h, V * h + V), w(sh, V * h, V * h + V), w("hs", 4 * V * h, 4 * V * h + 4 * V))
+        for c in range(3):
+            mm(bank(c, 0, 128), w(qh, 128 * c, 128 * c + 128), w(sh, 128 * c, 128 * c + 128), uq, us)
+        mm(bank(6), uq, us, w(qh, 0, V), w(sh, 0, V))
+        mm(bank(7), uq, us, w(qh, V, F), w(sh, V, F))
+        for c in range(3, 6):
+            mm(bank(c, 0, 128), w(qh, 128 * c, 128 * c + 128), w(sh, 128 * c, 128 * c + 128), uq, us)
+
+        def col(c):
+            return w("scol", c, c + 1)
+
+        def equal(c):
+            d = 128 * (c % 3)
+            fl = w("flags", 512 * c + V, 512 * c + 512)
+            ts(fl, bank(6 + c // 3, d, d + 128), col(c), 2.0, ALU.is_equal, ALU.mult)
+            op("g", lambda: g.affine_select(fl[0], fl[0], [[-1, 128]], ALU.is_gt, 0.0, 0, 1), fl, [fl])
+
+        def compare(c):
+            d = 128 * (c % 3)
+            if d:
+                ts(w("flags", 512 * c, 512 * c + d), bank(6 + c // 3, 0, d), col(c), 2.0, ALU.is_ge, ALU.mult)
+            ts(w("flags", 512 * c + d, 512 * c + V), bank(6 + c // 3, d, V), col(c), 2.0, ALU.is_gt, ALU.mult)
+
+        def count(c):
+            n = 384 if c == 5 else 256
+            scan(w("cnt", V * c + V - n, V * c + V), w("flags", 512 * c, 512 * c + n),
+                 w("flags", 512 * c + n, 512 * c + 2 * n), -256.0 if c == 5 else 0.0, ALU.add, ALU.add)
+
+        def sign1(c):
+            lo = 256 if c == 5 else 0
+            act(w("sg", V * c + lo, V * c + V), bank(7 - c // 3, lo, V), ACT.Sign, bias=col(c), scale=-1.0)
+
+        def sign2(c):
+            lo = 256 if c == 5 else 0
+            a = w("sg", V * c + lo, V * c + V)
+            act(a, a, ACT.Sign, bias=-0.5 if c < 3 else 0.5, scale=-1.0, accum=w("acc", c, c + 1))
+
+        act(w("scol", 0, 3), w("ps", 0, 1536, 512), ACT.Copy)
+        for c in range(3):
+            equal(c)
+        sign1(0)
+        act(w("scol", 3, 6), w("ps", 1536, 3072, 512), ACT.Copy)
+        sign1(1)
+        sign1(2)
+        for c in range(3):
+            compare(c)
+        ts(w("flags", 3072, 3328), bank(6, 0, 256), col(5), 2.0, ALU.is_ge, ALU.mult)
+        for c in range(3):
+            sign2(c)
+        for c in range(3, 6):
+            equal(c)
+        for c in range(3):
+            count(c)
+        for c in range(3, 6):
+            sign1(c)
+        for c in range(3, 6):
+            compare(c)
+        for c in range(3, 6):
+            sign2(c)
+        for c in range(3, 6):
+            count(c)
+        fo = "fo%d" % t
+        tt(w("tot", 0, 6), w("cnt", V - 1, 6 * V, V), w("acc", 0, 6), ALU.add)
+        ts(w("pos", 0, 6), w("tot", 0, 6), 0.5, 192.0, ALU.mult, ALU.add)
+        cp(by(w("pw"), w("pos", 0, 6)), w("fid"))
+        cp(w("p2"), by(w("pw", 0, K), w("dup")))
+        op("v", lambda: g.vector.transpose(T.tr[:], T.p2[:]), w("tr"), [w("p2")])
+        tt(w("u1", 0, 6), w("tr", 0, 192, 32), w("tr", 16, 192, 32), ALU.add)
+        tt(w("u2", 0, 6, 1, 0, 64), w("u1", 0, 6, 1, 0, 64), w("u1", 0, 6, 1, 64, 128), ALU.add)
+        for a in (0, 32):
+            tt(w("u3", 0, 6, 1, a, a + 32), w("u2", 0, 6, 1, 0, 32), w("u2", 0, 6, 1, 32, 64), ALU.add)
+        for a in (0, 64):
+            cp(w(fo, 0, 6, 1, a, a + 64), w("u3", 0, 6, 1, 0, 64))
+        remote(t, "list%d" % t, w("lst%d" % t), w(fo), mine[t][0])
+        cp(words(w("slotq%d" % t)), by(words(w(qh)), w(fo)))
+        act(w("slots%d" % t), by(w(sh), w(fo)), ACT.Copy)
+        remote(t, "data%d" % t, octets(w("landq%d" % t, 0, K)), octets(w("slotq%d" % t)), mine[t][1])
+        remote(t, "data%d" % t, w("lands%d" % t, 0, K), w("slots%d" % t), mine[t][0])
+        if t == 0:
+            cp(w("fvu"), w("fvi"))
+            act(w("fvrow"), by(w("num", 0, V), w("fvu")), ACT.Identity, bias=1.0)
+            for r in range(ROUNDS):
+                quant(w("landq%d" % r, K, K + 128), w("lands%d" % r, K, K + 128), w("xs", 0, 512))
+        act(w("flr%d" % t), by(w("num"), w(fo)), ACT.Copy)
+        dma("y", "dfl%d" % t, hbm(T.fl[t:t + 1, :]), w("flr%d" % t, 0, K, 1, 0, 1))
+        if t == 0:
+            spread_u(1, 3)
+        if t == 1:
+            quant(w("qwy"), w("swy"), w("wyb"))
+        if t < ROUNDS - 1:
+            fill(w("pw", 0, K), 0.0)
+        lst = w("lst%d" % t)
+        tt(w("gt"), by(w("fvrow"), lst), w("msk"), ALU.mult)
+        act(w("gu"), by(w("fvrow"), lst), ACT.Copy)
+        for e in range(4):
+            ts(w("f4", 6 * e, 6 * e + 6), lst, 4.0, float(e), ALU.mult, ALU.add)
+        act(w("x32"), by(w("hs"), w("f4")), ACT.Copy, scale=32.0)
+        scan(w("s1"), w("rmin"), w("gt"), 0.0, ALU.add, ALU.min)
+        for m in range(6):
+            ts(w("eq", K * m + 80, K * m + K), w("gt", 16 * m, 16 * m + 16), 1.0 / SPARE,
+               w("s1", 16 * m + 15, 16 * m + 16), ALU.mult, ALU.is_equal)
+        for m in range(1, 6):
+            ts(w("eq", K * m, K * m + 16 * m), w("gu", 0, 16 * m), 1.0 / SPARE,
+               w("s1", 16 * m + 15, 16 * m + 16), ALU.mult, ALU.is_equal)
+        scan(w("los"), w("rst"), w("eq"), 0.0, ALU.mult, ALU.add)
+        tt(w("dst", 0, 6), w("los", K - 1, 6 * K, K), w("s1", 15, K, 16), ALU.add)
+        for e in range(4):
+            ts(w("ob", 6 * e, 6 * e + 6), w("dst", 0, 6), 4.0 * SPARE, float(e - 4), ALU.mult, ALU.add)
+        for b in range(4):
+            mm(bank(b, 0, 128), w("qw", 128 * b, 128 * b + 128), w("sw", 128 * b, 128 * b + 128),
+               w("landq%d" % t, 0, 128), w("lands%d" % t, 0, 128))
+        for b in range(4):
+            tt(w("sm", K * b, K * b + K), bank(b, 0, K), w("x32", K * b, K * b + K), ALU.add)
+            if b == 1:
+                act(w("zb", 0, 2 * K), w("sm", 0, 2 * K), ACT.Copy, scale=0.015625)
+        ts(w("zb", 2 * K, 4 * K), w("sm", 2 * K, 4 * K), 0.015625, None, ALU.mult)
+        cp(by(w("xs"), w("ob")), w("zb"))
+
+    n = V // 2
+    for h in range(2):
+        quant(w("qx", n * h, n * h + n), w("sx", n * h, n * h + n), w("xs", 4 * n * h, 4 * n * h + 4 * n))
+        mm(bank(4 + h, 0, n), w("qwy"), w("swy"), w("qx", n * h, n * h + n), w("sx", n * h, n * h + n))
+        dma("y", "dout", hbm(T.oc[:, 4 * n * h:4 * n * h + 4 * n]), octets(w("qx", n * h, n * h + n)))
+    act(w("ysb", 0, n), bank(4, 0, n), ACT.Copy)
+    cp(w("ysb", n, V), bank(5, 0, n))
+    for h in range(2):
+        dma("s", "dy", hbm(T.y[:, n * h:n * h + n]), w("ysb", n * h, n * h + n))
+    for k in range(4):
+        dma("y", "dout", hbm(T.osc[4 * k:4 * k + 4, :]), w("sx", 0, V, 1, 32 * k, 32 * k + 4))
+    last = ["cp", "cs", "cv", "dout", "dy"]
+    for sem in [s for s in SEMAPHORES if s not in last] + last:
+        if total.get(sem, 0):
+            g.wait_ge(T.sem[sem], total[sem])

@@ -5,13 +5,15 @@ ACT = ActivationFunctionType
 V, F, K, ROUNDS = 384, 768, 96, 3
 SPARE = 512
 CODE = "float8_e4m3fn_x4"
+SEG = K + 2
+FW, CW = 896, 448
 
 SCRATCH = {
     "ps": ("psum", [128, 4096], "float32"),
     "fvi": ("sbuf", [128, 48], "int32"),
     "fvu": ("sbuf", [128, 48], "uint16"),
     "o4": ("sbuf", [128, 192], "uint16"),
-    "xs": ("sbuf", [128, 4 * (SPARE + V)], "bfloat16"),
+    "xs": ("sbuf", [128, 4 * V], "bfloat16"),
     "hs": ("sbuf", [128, 4 * F], "bfloat16"),
     "ub": ("sbuf", [128, 512], "bfloat16"),
     "qu": ("sbuf", [128, 128], CODE),
@@ -29,9 +31,10 @@ SCRATCH = {
     "ysb": ("sbuf", [128, V], "float32"),
     "scol": ("sbuf", [128, 8], "float32"),
     "acc": ("sbuf", [128, 8], "float32"),
-    "flags": ("sbuf", [128, 3328], "bfloat16"),
+    "acb": ("sbuf", [128, 8], "float32"),
+    "flags": ("sbuf", [128, 6 * FW], "bfloat16"),
     "sg": ("sbuf", [128, 2304], "bfloat16"),
-    "cnt": ("sbuf", [128, 2304], "float16"),
+    "cnt": ("sbuf", [128, 6 * CW], "float16"),
     "tot": ("sbuf", [128, 8], "float32"),
     "pos": ("sbuf", [128, 8], "uint16"),
     "pw": ("sbuf", [128, F], "float32"),
@@ -46,25 +49,28 @@ SCRATCH = {
     "pcol": ("sbuf", [128, 4], "float32"),
     "fid": ("sbuf", [128, K], "float32"),
     "dif": ("sbuf", [128, K], "float32"),
-    "m1": ("sbuf", [128, K], "float32"),
-    "m2": ("sbuf", [128, K], "float32"),
     "msk": ("sbuf", [128, K], "float32"),
-    "rmin": ("sbuf", [128, K], "float32"),
-    "rst": ("sbuf", [128, 6 * K], "bfloat16"),
+    "rst": ("sbuf", [128, K], "float32"),
+    "cci": ("sbuf", [128, 6 * SEG], "bfloat16"),
+    "cc": ("sbuf", [128, 6 * SEG], "bfloat16"),
     "dupi": ("sbuf", [128, 12], "float32"),
     "dup": ("sbuf", [128, 12], "uint16"),
+    "revi": ("sbuf", [128, 6], "float32"),
+    "rev": ("sbuf", [128, 6], "uint16"),
     "f4": ("sbuf", [128, 24], "uint16"),
-    "ob": ("sbuf", [128, 24], "uint16"),
+    "ob": ("sbuf", [128, 8], "uint16"),
     "gt": ("sbuf", [128, K], "float32"),
-    "gu": ("sbuf", [128, K], "float32"),
+    "gu": ("sbuf", [128, SEG + 2], "float32"),
     "s1": ("sbuf", [128, K], "float32"),
-    "eq": ("sbuf", [128, 6 * K], "bfloat16"),
-    "los": ("sbuf", [128, 6 * K], "bfloat16"),
+    "ne": ("sbuf", [128, 6 * SEG], "bfloat16"),
+    "win": ("sbuf", [128, 6 * SEG], "bfloat16"),
     "dst": ("sbuf", [128, 8], "float32"),
     "x32": ("sbuf", [128, 4 * K], "float32"),
-    "sm": ("sbuf", [128, 4 * K], "float32"),
     "zb": ("sbuf", [128, 4 * K], "bfloat16"),
+    "flb": ("sbuf", [128, K], "float32"),
 }
+for _t in range(4):
+    SCRATCH["xp%d" % _t] = ("sbuf", [128, SPARE + V], "bfloat16")
 for _t in range(ROUNDS):
     SCRATCH["qh%d" % _t] = ("sbuf", [128, F], CODE)
     SCRATCH["sh%d" % _t] = ("sbuf", [128, F], "uint8")
@@ -207,7 +213,9 @@ def rank_program(g, core, T, topo):
         op("v", lambda: g.vector.memset(out[0], c), out, [])
 
     def scan(out, a, b, init, op0, op1):
-        op("v", lambda: g.vector.tensor_tensor_scan(out[0], a[0], b[0], init, op0, op1), out, [a, b])
+        ins = [a, b] + ([init] if isinstance(init, tuple) else [])
+        x = init[0] if isinstance(init, tuple) else init
+        op("v", lambda: g.vector.tensor_tensor_scan(out[0], a[0], b[0], x, op0, op1), out, ins)
 
     def quant(codes, scales, a):
         op("v", lambda: g.vector.quantize_mx(codes[0], scales[0], a[0]), codes, [a], scales)
@@ -250,7 +258,7 @@ def rank_program(g, core, T, topo):
 
     dma("y", "dfv", w("fvi"), hbm(T.fv[:]))
     dma("s", "du", w("ub"), hbm(T.u[:]))
-    dma("y", "dx", w("xs", 0, 4 * V), hbm(T.x[:]))
+    dma("y", "dx", w("xs"), hbm(T.x[:]))
     wait("y", "dx", 16, {})
     dma("y", "dwc", octets(w("qw")), hbm(T.wc[:]))
     dma("y", "dws", w("sw"), hbm(T.ws[:]))
@@ -260,36 +268,36 @@ def rank_program(g, core, T, topo):
     iota(w("fid"), [[128, 6], [1, 16]], 0, 0)
     iota(w("dif"), [[0, 6], [1, 16]], 0, 0)
     iota(w("dupi"), [[16, 6], [0, 2]], 0, 0)
+    iota(w("revi"), [[-16, 6]], K - 1, 0)
     iota(w("num"), [[1, F]], 0, 0)
+    iota(w("cci"), [[-16, 6], [1, SEG]], 0, 0)
     for t in range(ROUNDS):
         fill(w("uoff", 8 * t, 8 * t + 8), t)
-    fill(w("pw", 0, K), 0.0)
-    fill(w("rmin"), 0.0)
+    fill(w("pw", F - K, F), 0.0)
     fill(w("rst"), 1.0)
-    fill(w("eq"), 0.0)
-    fill(w("rmin", 0, K, 16), 1.0e6)
-    fill(w("rst", 0, 6 * K, K), 0.0)
+    fill(w("ne"), 0.0)
+    fill(w("gu", K, SEG + 2), 0.0)
+    fill(w("acb"), 0.0)
+    fill(w("flags", FW + V, FW + V + 4), -32.0)
+    fill(w("rst", 0, K, 16), 0.0)
     ts(w("pidx", 1, 2), w("pidx", 0, 1), 15, None, ALU.bitwise_and)
     ts(w("pidx", 2, 3), w("pidx", 0, 1), 112, None, ALU.bitwise_and)
     cp(w("pcol", 0, 2), w("pidx", 1, 3))
     ts(w("fid"), w("fid"), w("pcol", 1, 2), None, ALU.add)
-    ts(w("dif"), w("dif"), w("pcol", 0, 1), None, ALU.subtract)
+    ts(w("msk"), w("dif"), w("pcol", 0, 1), None, ALU.is_equal)
     ts(w("dup"), w("dupi"), w("pcol", 0, 1), None, ALU.add)
-    ts(w("m1"), w("dif"), 0.0, 1.0 / SPARE, ALU.is_equal, ALU.mult)
-    ts(w("m2"), w("dif"), 0.0, 1024.0, ALU.is_gt, ALU.mult)
-    ts(w("msk"), w("dif"), 0.0, None, ALU.is_lt)
-    tt(w("m1"), w("m1"), w("m2"), ALU.add)
-    tt(w("msk"), w("msk"), w("m1"), ALU.add)
-    for e in range(4):
+    ts(w("rev"), w("revi"), w("pcol", 0, 1), None, ALU.subtract)
+    for e in (2, 3, 0, 1):
         ts(w("o4", 48 * e, 48 * e + 48), w("fvi"), 4.0, float(e), ALU.mult, ALU.add)
+    cp(w("fvu"), w("fvi"))
     quant(w("qu"), w("su"), w("ub"))
 
-    def spread_u(a, b):
-        off = w("uoff", 8 * a, 8 * b)
-        cp(words(w("ubc", 128 * a, 128 * b)), by(words(w("qu")), off))
-        act(w("sbc", 128 * a, 128 * b), by(w("su"), off), ACT.Copy)
+    def spread_u(a):
+        off = w("uoff", 8 * a, 8 * a + 8)
+        cp(words(w("ubc", 128 * a, 128 * a + 128)), by(words(w("qu")), off))
+        act(w("sbc", 128 * a, 128 * a + 128), by(w("su"), off), ACT.Copy)
 
-    spread_u(0, 1)
+    spread_u(0)
 
     def bank(b, lo=0, hi=V):
         return w("ps", 512 * b + lo, 512 * b + hi)
@@ -297,79 +305,112 @@ def rank_program(g, core, T, topo):
     for t in range(ROUNDS):
         qh, sh = "qh%d" % t, "sh%d" % t
         uq, us = w("ubc", 128 * t, 128 * t + 128), w("sbc", 128 * t, 128 * t + 128)
-        for e in range(4):
-            src = by(w("xs", 0, 4 * V), w("o4", 48 * e, 48 * e + 48))
-            if e < 2:
-                cp(w("hs", e, 4 * F, 4), src)
+
+        def gather(q, e, h):
+            out = w("hs", 4 * V * h + e, 4 * V * h + 4 * V, 4)
+            if t == 0:
+                src = by(w("xs"), w("o4", 48 * e + 24 * h, 48 * e + 24 * h + 24))
+                if q == "v":
+                    cp(out, src)
+                else:
+                    act(out, src, ACT.Copy)
             else:
-                act(w("hs", e, 4 * F, 4), src, ACT.Copy)
-        for h in range(2):
+                src = by(w("xp%d" % e, 0, V), w("fvu", 24 * h, 24 * h + 24))
+                if q == "v":
+                    ts(out, src, 0.015625, None, ALU.mult)
+                else:
+                    act(out, src, ACT.Copy, scale=0.015625)
+
+        def half(h):
             quant(w(qh, V * h, V * h + V), w(sh, V * h, V * h + V), w("hs", 4 * V * h, 4 * V * h + 4 * V))
-        for c in range(3):
-            mm(bank(c, 0, 128), w(qh, 128 * c, 128 * c + 128), w(sh, 128 * c, 128 * c + 128), uq, us)
-        mm(bank(6), uq, us, w(qh, 0, V), w(sh, 0, V))
-        mm(bank(7), uq, us, w(qh, V, F), w(sh, V, F))
-        for c in range(3, 6):
-            mm(bank(c, 0, 128), w(qh, 128 * c, 128 * c + 128), w(sh, 128 * c, 128 * c + 128), uq, us)
+            for c in range(3 * h, 3 * h + 3):
+                mm(bank(c % 3, 0, 128), w(qh, 128 * c, 128 * c + 128), w(sh, 128 * c, 128 * c + 128), uq, us)
+            for b in (4 + 2 * h, 3 + 2 * h):
+                mm(bank(b), uq, us, w(qh, V * h, V * h + V), w(sh, V * h, V * h + V))
 
         def col(c):
             return w("scol", c, c + 1)
 
+        mine_v = {0: [(0, 0, 128, ALU.is_gt)], 1: [(0, 128, 384, ALU.is_gt)], 2: [(0, 256, 384, ALU.is_gt)],
+                  3: [(1, 0, 384, ALU.is_gt)],
+                  4: [(0, 0, 256, ALU.is_ge), (1, 0, 128, ALU.is_ge), (1, 128, 384, ALU.is_gt)],
+                  5: [(0, 0, 384, ALU.is_ge), (1, 0, 256, ALU.is_ge), (1, 256, 384, ALU.is_gt)]}
+        early = [(0, 0, 128, 384, False, "acc"), (1, 0, 0, 128, True, "acc"), (2, 0, 0, 256, True, "acc")]
+        late = [(0, 1, 0, 384, False, "acb"), (1, 1, 0, 384, False, "acb"), (2, 1, 0, 384, False, "acb"),
+                (3, 0, 0, 384, True, "acb"), (4, 0, 256, 384, True, "acb")]
+        place = {}
+        at = 0
+        for j in early + late:
+            place[j] = at
+            at += j[3] - j[2]
+
         def equal(c):
             d = 128 * (c % 3)
-            fl = w("flags", 512 * c + V, 512 * c + 512)
-            ts(fl, bank(6 + c // 3, d, d + 128), col(c), 2.0, ALU.is_equal, ALU.mult)
+            fl = w("flags", FW * c, FW * c + 128)
+            ts(fl, bank(3 + 2 * (c // 3), d, d + 128), col(c), 2.0, ALU.is_equal, ALU.mult)
             op("g", lambda: g.affine_select(fl[0], fl[0], [[-1, 128]], ALU.is_gt, 0.0, 0, 1), fl, [fl])
 
-        def compare(c):
-            d = 128 * (c % 3)
-            if d:
-                ts(w("flags", 512 * c, 512 * c + d), bank(6 + c // 3, 0, d), col(c), 2.0, ALU.is_ge, ALU.mult)
-            ts(w("flags", 512 * c + d, 512 * c + V), bank(6 + c // 3, d, V), col(c), 2.0, ALU.is_gt, ALU.mult)
+        def compare(c, which):
+            a = FW * c + 128
+            for i, (h, lo, hi, o) in enumerate(mine_v[c]):
+                if i in which:
+                    ts(w("flags", a, a + hi - lo), bank(3 + 2 * h, lo, hi), col(c), 2.0, o, ALU.mult)
+                a += hi - lo
 
         def count(c):
-            n = 384 if c == 5 else 256
-            scan(w("cnt", V * c + V - n, V * c + V), w("flags", 512 * c, 512 * c + n),
-                 w("flags", 512 * c + n, 512 * c + 2 * n), -256.0 if c == 5 else 0.0, ALU.add, ALU.add)
+            n = (128 + sum(j[2] - j[1] for j in mine_v[c]) + (4 if c == 1 else 0)) // 2
+            init = w("acc", c, c + 1) if c < 3 else (-256.0, -512.0, -640.0)[c - 3]
+            scan(w("cnt", CW * c + CW - n, CW * c + CW), w("flags", FW * c, FW * c + n),
+                 w("flags", FW * c + n, FW * c + 2 * n), init, ALU.add, ALU.add)
 
-        def sign1(c):
-            lo = 256 if c == 5 else 0
-            act(w("sg", V * c + lo, V * c + V), bank(7 - c // 3, lo, V), ACT.Sign, bias=col(c), scale=-1.0)
+        def sign1(j):
+            act(w("sg", place[j], place[j] + j[3] - j[2]), bank(4 + 2 * j[1], j[2], j[3]), ACT.Sign, bias=col(j[0]), scale=-1.0)
 
-        def sign2(c):
-            lo = 256 if c == 5 else 0
-            a = w("sg", V * c + lo, V * c + V)
-            act(a, a, ACT.Sign, bias=-0.5 if c < 3 else 0.5, scale=-1.0, accum=w("acc", c, c + 1))
+        def sign2(j):
+            a = w("sg", place[j], place[j] + j[3] - j[2])
+            act(a, a, ACT.Sign, bias=0.5 if j[4] else -0.5, scale=-1.0, accum=w(j[5], j[0], j[0] + 1))
 
+        first = ([0, 1], [2, 3]) if t == 0 else ([3], [0, 1, 2])
+        second = ([0, 1], [2, 3]) if t == 0 else ([3, 2], [0, 1])
+        for e in first[1]:
+            gather("s", e, 0)
+        for e in first[0]:
+            gather("v", e, 0)
+        for e in second[1]:
+            gather("s", e, 1)
+        half(0)
         act(w("scol", 0, 3), w("ps", 0, 1536, 512), ACT.Copy)
+        for e in second[0]:
+            gather("v", e, 1)
+        half(1)
+        for j in early:
+            sign1(j)
+        for j in early:
+            sign2(j)
+        act(w("scol", 3, 6), w("ps", 0, 1536, 512), ACT.Copy)
         for c in range(3):
             equal(c)
-        sign1(0)
-        act(w("scol", 3, 6), w("ps", 1536, 3072, 512), ACT.Copy)
-        sign1(1)
-        sign1(2)
         for c in range(3):
-            compare(c)
-        ts(w("flags", 3072, 3328), bank(6, 0, 256), col(5), 2.0, ALU.is_ge, ALU.mult)
-        for c in range(3):
-            sign2(c)
+            compare(c, [0])
         for c in range(3, 6):
             equal(c)
         for c in range(3):
             count(c)
-        for c in range(3, 6):
-            sign1(c)
-        for c in range(3, 6):
-            compare(c)
-        for c in range(3, 6):
-            sign2(c)
-        for c in range(3, 6):
-            count(c)
+        for j in late:
+            sign1(j)
+        for j in late:
+            sign2(j)
+        compare(3, [0])
+        compare(4, [0, 1, 2])
+        count(3)
+        compare(5, [0, 1, 2])
+        count(4)
+        count(5)
         fo = "fo%d" % t
-        tt(w("tot", 0, 6), w("cnt", V - 1, 6 * V, V), w("acc", 0, 6), ALU.add)
-        ts(w("pos", 0, 6), w("tot", 0, 6), 0.5, 192.0, ALU.mult, ALU.add)
+        tt(w("tot", 0, 6), w("cnt", CW - 1, 6 * CW, CW), w("acb", 0, 6), ALU.add)
+        ts(w("pos", 0, 6), w("tot", 0, 6), -0.5, float(F - 1 - 320), ALU.mult, ALU.add)
         cp(by(w("pw"), w("pos", 0, 6)), w("fid"))
-        cp(w("p2"), by(w("pw", 0, K), w("dup")))
+        cp(w("p2"), by(w("pw", F - K, F), w("dup")))
         op("v", lambda: g.vector.transpose(T.tr[:], T.p2[:]), w("tr"), [w("p2")])
         tt(w("u1", 0, 6), w("tr", 0, 192, 32), w("tr", 16, 192, 32), ALU.add)
         tt(w("u2", 0, 6, 1, 0, 64), w("u1", 0, 6, 1, 0, 64), w("u1", 0, 6, 1, 64, 128), ALU.add)
@@ -383,45 +424,52 @@ def rank_program(g, core, T, topo):
         remote(t, "data%d" % t, octets(w("landq%d" % t, 0, K)), octets(w("slotq%d" % t)), mine[t][1])
         remote(t, "data%d" % t, w("lands%d" % t, 0, K), w("slots%d" % t), mine[t][0])
         if t == 0:
-            cp(w("fvu"), w("fvi"))
             act(w("fvrow"), by(w("num", 0, V), w("fvu")), ACT.Identity, bias=1.0)
-            for r in range(ROUNDS):
-                quant(w("landq%d" % r, K, K + 128), w("lands%d" % r, K, K + 128), w("xs", 0, 512))
-        act(w("flr%d" % t), by(w("num"), w(fo)), ACT.Copy)
-        dma("y", "dfl%d" % t, hbm(T.fl[t:t + 1, :]), w("flr%d" % t, 0, K, 1, 0, 1))
+            ts(w("cc"), w("cci"), w("pcol", 0, 1), 1.5, ALU.subtract, ALU.is_le)
+        quant(w("landq%d" % t, K, K + 128), w("lands%d" % t, K, K + 128), w("xs", 0, 512))
         if t == 0:
-            spread_u(1, 3)
+            for e in range(4):
+                ts(w("xp%d" % e, 0, V), w("xs", e, 4 * V, 4), 64.0, None, ALU.mult)
+        if t < ROUNDS - 1:
+            spread_u(t + 1)
+            fill(w("pw", F - K, F), 0.0)
         if t == 1:
             quant(w("qwy"), w("swy"), w("wyb"))
-        if t < ROUNDS - 1:
-            fill(w("pw", 0, K), 0.0)
         lst = w("lst%d" % t)
         tt(w("gt"), by(w("fvrow"), lst), w("msk"), ALU.mult)
-        act(w("gu"), by(w("fvrow"), lst), ACT.Copy)
-        for e in range(4):
+        act(w("gu", 0, K), by(w("fvrow"), lst), ACT.Copy)
+        for e in range(2):
+            ts(w("f4", 6 * e, 6 * e + 6), lst, 4.0, float(e), ALU.mult, ALU.add)
+        scan(w("s1"), w("rst"), w("gt"), 0.0, ALU.mult, ALU.add)
+        for e in range(2, 4):
             ts(w("f4", 6 * e, 6 * e + 6), lst, 4.0, float(e), ALU.mult, ALU.add)
         act(w("x32"), by(w("hs"), w("f4")), ACT.Copy, scale=32.0)
-        scan(w("s1"), w("rmin"), w("gt"), 0.0, ALU.add, ALU.min)
         for m in range(6):
-            ts(w("eq", K * m + 80, K * m + K), w("gt", 16 * m, 16 * m + 16), 1.0 / SPARE,
-               w("s1", 16 * m + 15, 16 * m + 16), ALU.mult, ALU.is_equal)
-        for m in range(1, 6):
-            ts(w("eq", K * m, K * m + 16 * m), w("gu", 0, 16 * m), 1.0 / SPARE,
-               w("s1", 16 * m + 15, 16 * m + 16), ALU.mult, ALU.is_equal)
-        scan(w("los"), w("rst"), w("eq"), 0.0, ALU.mult, ALU.add)
-        tt(w("dst", 0, 6), w("los", K - 1, 6 * K, K), w("s1", 15, K, 16), ALU.add)
-        for e in range(4):
-            ts(w("ob", 6 * e, 6 * e + 6), w("dst", 0, 6), 4.0 * SPARE, float(e - 4), ALU.mult, ALU.add)
+            ts(w("ne", SEG * m + 16 * m, SEG * m + SEG), w("gu", 16 * m, SEG), w("s1", 16 * m + 15, 16 * m + 16), None,
+               ALU.not_equal)
+        scan(w("win"), w("cc"), w("ne"), 0.0, ALU.max, ALU.min)
         for b in range(4):
             mm(bank(b, 0, 128), w("qw", 128 * b, 128 * b + 128), w("sw", 128 * b, 128 * b + 128),
                w("landq%d" % t, 0, 128), w("lands%d" % t, 0, 128))
-        for b in range(4):
-            tt(w("sm", K * b, K * b + K), bank(b, 0, K), w("x32", K * b, K * b + K), ALU.add)
-            if b == 1:
-                act(w("zb", 0, 2 * K), w("sm", 0, 2 * K), ACT.Copy, scale=0.015625)
-        ts(w("zb", 2 * K, 4 * K), w("sm", 2 * K, 4 * K), 0.015625, None, ALU.mult)
-        cp(by(w("xs"), w("ob")), w("zb"))
+        ts(w("u1", 0, 6), w("s1", 15, K, 16), 1.0 / SPARE, None, ALU.mult)
+        tt(w("dst", 0, 6), w("u1", 0, 6), w("win", SEG - 1, 6 * SEG, SEG), ALU.subtract)
 
+        def blend(b):
+            tt(w("zb", K * b, K * b + K), bank(b, 0, K), w("x32", K * b, K * b + K), ALU.add)
+
+        ts(w("ob", 0, 6), w("dst", 0, 6), float(SPARE), float(SPARE - 1), ALU.mult, ALU.add)
+        blend(0)
+        for b in range(4):
+            if b < 3:
+                blend(b + 1)
+            cp(by(w("xp%d" % b), w("ob", 0, 6)), w("zb", K * b, K * b + K))
+        act(w("flb"), by(w("num"), w(fo)), ACT.Copy)
+        act(w("flr%d" % t), by(w("flb"), w("rev")), ACT.Copy)
+        dma("y", "dfl%d" % t, hbm(T.fl[t:t + 1, :]), w("flr%d" % t, 0, K, 1, 0, 1))
+
+    for e in range(3):
+        act(w("xs", e, 4 * V, 4), w("xp%d" % e, 0, V), ACT.Copy, scale=0.015625)
+    ts(w("xs", 3, 4 * V, 4), w("xp3", 0, V), 0.015625, None, ALU.mult)
     n = V // 2
     for h in range(2):
         quant(w("qx", n * h, n * h + n), w("sx", n * h, n * h + n), w("xs", 4 * n * h, 4 * n * h + 4 * n))

@@ -3,10 +3,12 @@ from concourse.mybir import dt, AluOpType, ActivationFunctionType
 ALU = AluOpType
 ACT = ActivationFunctionType
 V, F, K, ROUNDS = 384, 768, 96, 3
-SPARE = 512
+HOME = 512
 CODE = "float8_e4m3fn_x4"
 SEG = K + 2
-FW, CW = 896, 448
+FW, CW = 768, 384
+STEP = 0.625 * 2.0 ** -23
+TINY = 2.0 ** -120
 
 SCRATCH = {
     "ps": ("psum", [128, 4096], "float32"),
@@ -30,31 +32,32 @@ SCRATCH = {
     "sx": ("sbuf", [128, V], "uint8"),
     "ysb": ("sbuf", [128, V], "float32"),
     "scol": ("sbuf", [128, 8], "float32"),
+    "gap": ("sbuf", [128, 8], "float32"),
+    "tri": ("sbuf", [128, 128], "bfloat16"),
+    "bar": ("sbuf", [128, F], "float32"),
     "acc": ("sbuf", [128, 8], "float32"),
     "acb": ("sbuf", [128, 8], "float32"),
     "flags": ("sbuf", [128, 6 * FW], "bfloat16"),
     "sg": ("sbuf", [128, 2304], "bfloat16"),
     "cnt": ("sbuf", [128, 6 * CW], "float16"),
-    "tot": ("sbuf", [128, 8], "float32"),
     "pos": ("sbuf", [128, 8], "uint16"),
-    "pw": ("sbuf", [128, F], "float32"),
-    "p2": ("sbuf", [128, 192], "float32"),
-    "tr": ("sbuf", [128, 192], "float32"),
+    "pw": ("sbuf", [128, F + 16], "float32"),
+    "tra": ("sbuf", [128, 96], "float32"),
+    "trc": ("sbuf", [128, 128], "float32"),
     "u1": ("sbuf", [128, 8], "float32"),
     "u2": ("sbuf", [128, 8], "float32"),
     "u3": ("sbuf", [128, 8], "float32"),
     "num": ("sbuf", [128, F], "float32"),
     "fvrow": ("sbuf", [128, F], "float32"),
     "pidx": ("sbuf", [128, 4], "int32"),
-    "pcol": ("sbuf", [128, 4], "float32"),
+    "pcol": ("sbuf", [128, 8], "float32"),
     "fid": ("sbuf", [128, K], "float32"),
     "dif": ("sbuf", [128, K], "float32"),
     "msk": ("sbuf", [128, K], "float32"),
     "rst": ("sbuf", [128, K], "float32"),
     "cci": ("sbuf", [128, 6 * SEG], "bfloat16"),
-    "cc": ("sbuf", [128, 6 * SEG], "bfloat16"),
-    "dupi": ("sbuf", [128, 12], "float32"),
-    "dup": ("sbuf", [128, 12], "uint16"),
+    "cc": ("sbuf", [128, 6 * SEG], "float16"),
+    "turn": ("sbuf", [128, 2], "uint16"),
     "revi": ("sbuf", [128, 6], "float32"),
     "rev": ("sbuf", [128, 6], "uint16"),
     "f4": ("sbuf", [128, 24], "uint16"),
@@ -62,19 +65,18 @@ SCRATCH = {
     "gt": ("sbuf", [128, K], "float32"),
     "gu": ("sbuf", [128, SEG + 2], "float32"),
     "s1": ("sbuf", [128, K], "float32"),
-    "ne": ("sbuf", [128, 6 * SEG], "bfloat16"),
-    "win": ("sbuf", [128, 6 * SEG], "bfloat16"),
-    "dst": ("sbuf", [128, 8], "float32"),
+    "ne": ("sbuf", [128, 6 * SEG], "float16"),
+    "win": ("sbuf", [128, 6 * SEG], "float16"),
     "x32": ("sbuf", [128, 4 * K], "float32"),
     "zb": ("sbuf", [128, 4 * K], "bfloat16"),
     "flb": ("sbuf", [128, K], "float32"),
 }
 for _t in range(4):
-    SCRATCH["xp%d" % _t] = ("sbuf", [128, SPARE + V], "bfloat16")
+    SCRATCH["xp%d" % _t] = ("sbuf", [128, HOME + V], "bfloat16")
 for _t in range(ROUNDS):
     SCRATCH["qh%d" % _t] = ("sbuf", [128, F], CODE)
     SCRATCH["sh%d" % _t] = ("sbuf", [128, F], "uint8")
-    SCRATCH["fo%d" % _t] = ("sbuf", [128, 6], "uint16")
+    SCRATCH["fo%d" % _t] = ("sbuf", [128, 16], "uint16")
     SCRATCH["lst%d" % _t] = ("sbuf", [128, 6], "uint16")
     SCRATCH["slotq%d" % _t] = ("sbuf", [128, K], CODE)
     SCRATCH["slots%d" % _t] = ("sbuf", [128, K], "uint8")
@@ -212,6 +214,9 @@ def rank_program(g, core, T, topo):
     def fill(out, c):
         op("v", lambda: g.vector.memset(out[0], c), out, [])
 
+    def turn(out, a):
+        op("v", lambda: g.vector.transpose(out[0], a[0]), out, [a])
+
     def scan(out, a, b, init, op0, op1):
         ins = [a, b] + ([init] if isinstance(init, tuple) else [])
         x = init[0] if isinstance(init, tuple) else init
@@ -223,12 +228,11 @@ def rank_program(g, core, T, topo):
     def act(out, a, func, bias=None, scale=None, accum=None):
         kw = {}
         ins = [a]
-        if bias is not None:
-            kw["bias"] = bias[0] if isinstance(bias, tuple) else bias
-            if isinstance(bias, tuple):
-                ins.append(bias)
-        if scale is not None:
-            kw["scale"] = scale
+        for name, x in (("bias", bias), ("scale", scale)):
+            if x is not None:
+                kw[name] = x[0] if isinstance(x, tuple) else x
+                if isinstance(x, tuple):
+                    ins.append(x)
         if accum is not None:
             kw["accum_out"] = accum[0]
         op("s", lambda: g.scalar.activation(out[0], a[0], func, **kw), out, ins, accum)
@@ -257,9 +261,9 @@ def rank_program(g, core, T, topo):
         log.append((w("lands%d" % t, 0, K)[1][0], True, "far", "data%d" % t, a + b, {}))
 
     dma("y", "dfv", w("fvi"), hbm(T.fv[:]))
-    dma("s", "du", w("ub"), hbm(T.u[:]))
     dma("y", "dx", w("xs"), hbm(T.x[:]))
-    wait("y", "dx", 16, {})
+    dma("y", "du", w("ub"), hbm(T.u[:]))
+    wait("y", "du", 16, {})
     dma("y", "dwc", octets(w("qw")), hbm(T.wc[:]))
     dma("y", "dws", w("sw"), hbm(T.ws[:]))
     dma("y", "dwy", w("wyb"), hbm(T.wy[:]))
@@ -267,37 +271,37 @@ def rank_program(g, core, T, topo):
     iota(w("pidx", 0, 1), [[0, 1]], 0, 1, small=False)
     iota(w("fid"), [[128, 6], [1, 16]], 0, 0)
     iota(w("dif"), [[0, 6], [1, 16]], 0, 0)
-    iota(w("dupi"), [[16, 6], [0, 2]], 0, 0)
     iota(w("revi"), [[-16, 6]], K - 1, 0)
+    fill(w("tri"), 1.0)
+    op("g", lambda: g.affine_select(T.tri[:], T.tri[:], [[1, 128]], ALU.is_gt, 0.0, 0, -1), w("tri"), [w("tri")])
     iota(w("num"), [[1, F]], 0, 0)
     iota(w("cci"), [[-16, 6], [1, SEG]], 0, 0)
     for t in range(ROUNDS):
         fill(w("uoff", 8 * t, 8 * t + 8), t)
-    fill(w("pw", F - K, F), 0.0)
+    fill(w("pw", F - K - 16, F + 16), 0.0)
     fill(w("rst"), 1.0)
     fill(w("ne"), 0.0)
-    fill(w("gu", K, SEG + 2), 0.0)
-    fill(w("acb"), 0.0)
-    fill(w("flags", FW + V, FW + V + 4), -32.0)
+    fill(w("gu", K, SEG + 2), -1.0)
+    fill(w("u3"), 0.0)
     fill(w("rst", 0, K, 16), 0.0)
     ts(w("pidx", 1, 2), w("pidx", 0, 1), 15, None, ALU.bitwise_and)
     ts(w("pidx", 2, 3), w("pidx", 0, 1), 112, None, ALU.bitwise_and)
-    cp(w("pcol", 0, 2), w("pidx", 1, 3))
+    ts(w("pidx", 3, 4), w("pidx", 0, 1), 16, None, ALU.bitwise_and)
+    cp(w("pcol", 0, 3), w("pidx", 1, 4))
     ts(w("fid"), w("fid"), w("pcol", 1, 2), None, ALU.add)
     ts(w("msk"), w("dif"), w("pcol", 0, 1), None, ALU.is_equal)
-    ts(w("dup"), w("dupi"), w("pcol", 0, 1), None, ALU.add)
     ts(w("rev"), w("revi"), w("pcol", 0, 1), None, ALU.subtract)
-    for e in (2, 3, 0, 1):
+    ts(w("pcol", 3, 4), w("pcol", 2, 3), -0.0625, 1.0, ALU.mult, ALU.add)
+    ts(w("pcol", 4, 5), w("pcol", 0, 1), 1.5, None, ALU.add)
+    ts(w("turn", 0, 1), w("pcol", 3, 4), w("pcol", 0, 1), 7.0, ALU.add, ALU.min)
+    for e in (1, 2, 3, 0):
         ts(w("o4", 48 * e, 48 * e + 48), w("fvi"), 4.0, float(e), ALU.mult, ALU.add)
     cp(w("fvu"), w("fvi"))
-    quant(w("qu"), w("su"), w("ub"))
 
     def spread_u(a):
         off = w("uoff", 8 * a, 8 * a + 8)
         cp(words(w("ubc", 128 * a, 128 * a + 128)), by(words(w("qu")), off))
         act(w("sbc", 128 * a, 128 * a + 128), by(w("su"), off), ACT.Copy)
-
-    spread_u(0)
 
     def bank(b, lo=0, hi=V):
         return w("ps", 512 * b + lo, 512 * b + hi)
@@ -315,7 +319,7 @@ def rank_program(g, core, T, topo):
                 else:
                     act(out, src, ACT.Copy)
             else:
-                src = by(w("xp%d" % e, 0, V), w("fvu", 24 * h, 24 * h + 24))
+                src = by(w("xp%d" % e, HOME, HOME + V), w("fvu", 24 * h, 24 * h + 24))
                 if q == "v":
                     ts(out, src, 0.015625, None, ALU.mult)
                 else:
@@ -325,41 +329,44 @@ def rank_program(g, core, T, topo):
             quant(w(qh, V * h, V * h + V), w(sh, V * h, V * h + V), w("hs", 4 * V * h, 4 * V * h + 4 * V))
             for c in range(3 * h, 3 * h + 3):
                 mm(bank(c % 3, 0, 128), w(qh, 128 * c, 128 * c + 128), w(sh, 128 * c, 128 * c + 128), uq, us)
-            for b in (4 + 2 * h, 3 + 2 * h):
+            for b in ((3, 4), (6, 5))[h]:
                 mm(bank(b), uq, us, w(qh, V * h, V * h + V), w(sh, V * h, V * h + V))
 
         def col(c):
             return w("scol", c, c + 1)
 
-        mine_v = {0: [(0, 0, 128, ALU.is_gt)], 1: [(0, 128, 384, ALU.is_gt)], 2: [(0, 256, 384, ALU.is_gt)],
-                  3: [(1, 0, 384, ALU.is_gt)],
-                  4: [(0, 0, 256, ALU.is_ge), (1, 0, 128, ALU.is_ge), (1, 128, 384, ALU.is_gt)],
-                  5: [(0, 0, 384, ALU.is_ge), (1, 0, 256, ALU.is_ge), (1, 256, 384, ALU.is_gt)]}
-        early = [(0, 0, 128, 384, False, "acc"), (1, 0, 0, 128, True, "acc"), (2, 0, 0, 256, True, "acc")]
-        late = [(0, 1, 0, 384, False, "acb"), (1, 1, 0, 384, False, "acb"), (2, 1, 0, 384, False, "acb"),
-                (3, 0, 0, 384, True, "acb"), (4, 0, 256, 384, True, "acb")]
+        lt, le = ALU.is_lt, ALU.is_le
+        mine_v = {0: [(0, 128, 384, le)], 1: [(0, 0, 128, lt), (0, 256, 384, le)], 2: [],
+                  3: [(0, 0, 384, lt), (1, 128, 384, le)],
+                  4: [(0, 0, 384, lt), (1, 0, 128, lt), (1, 256, 384, le)],
+                  5: [(0, 0, 384, lt), (1, 0, 256, lt)]}
+        early = [(2, 0, 0, 256, False, "acc")]
+        late = [(0, 1, 0, 384, True, "acb"), (1, 1, 0, 384, True, "acb"), (2, 1, 0, 384, True, "acb")]
         place = {}
         at = 0
         for j in early + late:
             place[j] = at
             at += j[3] - j[2]
 
-        def equal(c):
+        def bars(h, src):
+            act(w("gap", 3 * h, 3 * h + 3), src, ACT.Abs, bias=TINY, scale=STEP)
+            for c in range(3 * h, 3 * h + 3):
+                act(w("bar", 128 * c, 128 * c + 128), w("tri"), ACT.Identity, bias=col(c), scale=w("gap", c, c + 1))
+
+        def block(c):
             d = 128 * (c % 3)
-            fl = w("flags", FW * c, FW * c + 128)
-            ts(fl, bank(3 + 2 * (c // 3), d, d + 128), col(c), 2.0, ALU.is_equal, ALU.mult)
-            op("g", lambda: g.affine_select(fl[0], fl[0], [[-1, 128]], ALU.is_gt, 0.0, 0, 1), fl, [fl])
+            tt(w("flags", FW * c, FW * c + 128), bank(3 + 2 * (c // 3), d, d + 128), w("bar", 128 * c, 128 * c + 128), lt)
 
         def compare(c, which):
             a = FW * c + 128
             for i, (h, lo, hi, o) in enumerate(mine_v[c]):
                 if i in which:
-                    ts(w("flags", a, a + hi - lo), bank(3 + 2 * h, lo, hi), col(c), 2.0, o, ALU.mult)
+                    ts(w("flags", a, a + hi - lo), bank(3 + 2 * h, lo, hi), col(c), None, o)
                 a += hi - lo
 
         def count(c):
-            n = (128 + sum(j[2] - j[1] for j in mine_v[c]) + (4 if c == 1 else 0)) // 2
-            init = w("acc", c, c + 1) if c < 3 else (-256.0, -512.0, -640.0)[c - 3]
+            n = (128 + sum(j[2] - j[1] for j in mine_v[c])) // 2
+            init = w("acc", c, c + 1) if any(j[0] == c for j in early) else 0.0
             scan(w("cnt", CW * c + CW - n, CW * c + CW), w("flags", FW * c, FW * c + n),
                  w("flags", FW * c + n, FW * c + 2 * n), init, ALU.add, ALU.add)
 
@@ -368,73 +375,95 @@ def rank_program(g, core, T, topo):
 
         def sign2(j):
             a = w("sg", place[j], place[j] + j[3] - j[2])
-            act(a, a, ACT.Sign, bias=0.5 if j[4] else -0.5, scale=-1.0, accum=w(j[5], j[0], j[0] + 1))
+            if j[4]:
+                act(a, a, ACT.Sign, bias=1.0, accum=w(j[5], j[0], j[0] + 1))
+            else:
+                act(a, a, ACT.Relu, accum=w(j[5], j[0], j[0] + 1))
 
-        first = ([0, 1], [2, 3]) if t == 0 else ([3], [0, 1, 2])
-        second = ([0, 1], [2, 3]) if t == 0 else ([3, 2], [0, 1])
-        for e in first[1]:
-            gather("s", e, 0)
-        for e in first[0]:
-            gather("v", e, 0)
-        for e in second[1]:
-            gather("s", e, 1)
+        def spot(c):
+            ts(w("pos", c, c + 1), w("cnt", CW * c + CW - 1, CW * c + CW), w("acb", c, c + 1), None, ALU.add)
+
+        if t == 0:
+            gather("s", 1, 0)
+            gather("v", 0, 0)
+            gather("s", 2, 0)
+            quant(w("qu"), w("su"), w("ub"))
+            gather("v", 3, 0)
+            spread_u(0)
+        else:
+            for e in range(3):
+                gather("s", e, 0)
+            gather("v", 3, 0)
+        gather("s", 0, 1)
+        gather("s", 1, 1)
         half(0)
-        act(w("scol", 0, 3), w("ps", 0, 1536, 512), ACT.Copy)
-        for e in second[0]:
-            gather("v", e, 1)
+        gather("v", 3, 1)
+        gather("s", 2, 1)
+        cp(w("scol", 0, 3), w("ps", 0, 1536, 512))
+        bars(0, w("scol", 0, 3))
+        compare(0, [0])
+        compare(1, [0, 1])
         half(1)
         for j in early:
             sign1(j)
         for j in early:
             sign2(j)
         act(w("scol", 3, 6), w("ps", 0, 1536, 512), ACT.Copy)
+        bars(1, w("ps", 0, 1536, 512))
         for c in range(3):
-            equal(c)
-        for c in range(3):
-            compare(c, [0])
-        for c in range(3, 6):
-            equal(c)
+            block(c)
         for c in range(3):
             count(c)
-        for j in late:
-            sign1(j)
-        for j in late:
-            sign2(j)
-        compare(3, [0])
-        compare(4, [0, 1, 2])
+        sign1(late[0])
+        sign1(late[1])
+        sign2(late[0])
+        sign1(late[2])
+        sign2(late[1])
+        sign2(late[2])
+        for c in range(3, 6):
+            compare(c, [0])
+        for c in range(3, 6):
+            block(c)
+        compare(3, [1])
+        compare(4, [1, 2])
         count(3)
-        compare(5, [0, 1, 2])
+        compare(5, [1])
         count(4)
+        spot(0)
         count(5)
-        fo = "fo%d" % t
-        tt(w("tot", 0, 6), w("cnt", CW - 1, 6 * CW, CW), w("acb", 0, 6), ALU.add)
-        ts(w("pos", 0, 6), w("tot", 0, 6), -0.5, float(F - 1 - 320), ALU.mult, ALU.add)
+        spot(1)
+        spot(2)
+        fo = w("fo%d" % t, 0, 6)
+        cp(w("pos", 3, 6), w("cnt", 4 * CW - 1, 6 * CW, CW))
         cp(by(w("pw"), w("pos", 0, 6)), w("fid"))
-        cp(w("p2"), by(w("pw", F - K, F), w("dup")))
-        op("v", lambda: g.vector.transpose(T.tr[:], T.p2[:]), w("tr"), [w("p2")])
-        tt(w("u1", 0, 6), w("tr", 0, 192, 32), w("tr", 16, 192, 32), ALU.add)
-        tt(w("u2", 0, 6, 1, 0, 64), w("u1", 0, 6, 1, 0, 64), w("u1", 0, 6, 1, 64, 128), ALU.add)
-        for a in (0, 32):
-            tt(w("u3", 0, 6, 1, a, a + 32), w("u2", 0, 6, 1, 0, 32), w("u2", 0, 6, 1, 32, 64), ALU.add)
-        for a in (0, 64):
-            cp(w(fo, 0, 6, 1, a, a + 64), w("u3", 0, 6, 1, 0, 64))
-        remote(t, "list%d" % t, w("lst%d" % t), w(fo), mine[t][0])
-        cp(words(w("slotq%d" % t)), by(words(w(qh)), w(fo)))
-        act(w("slots%d" % t), by(w(sh), w(fo)), ACT.Copy)
+        turn(w("trc"), w("pw", F - K - 16, F + 16))
+        turn(w("tra"), w("pw", F - K, F))
+        tt(w("u1", 0, 7, 2), w("trc", 0, 128, 32), w("trc", 16, 128, 32), ALU.add)
+        tt(w("u1", 1, 7, 2), w("tra", 0, 96, 32), w("tra", 16, 96, 32), ALU.add)
+        tt(w("u2", 0, 7, 1, 0, 64), w("u1", 0, 7, 1, 0, 64), w("u1", 0, 7, 1, 64, 128), ALU.add)
+        for a in (0, 32, 64, 96):
+            tt(w("u3", 0, 7, 1, a, a + 32), w("u2", 0, 7, 1, 0, 32), w("u2", 0, 7, 1, 32, 64), ALU.add)
+        cp(w("fo%d" % t), by(w("u3"), w("turn", 0, 1)))
+        remote(t, "list%d" % t, w("lst%d" % t), fo, mine[t][0])
+        cp(words(w("slotq%d" % t)), by(words(w(qh)), fo))
+        act(w("slots%d" % t), by(w(sh), fo), ACT.Copy)
         remote(t, "data%d" % t, octets(w("landq%d" % t, 0, K)), octets(w("slotq%d" % t)), mine[t][1])
         remote(t, "data%d" % t, w("lands%d" % t, 0, K), w("slots%d" % t), mine[t][0])
         if t == 0:
-            act(w("fvrow"), by(w("num", 0, V), w("fvu")), ACT.Identity, bias=1.0)
-            ts(w("cc"), w("cci"), w("pcol", 0, 1), 1.5, ALU.subtract, ALU.is_le)
+            act(w("fvrow"), by(w("num", 0, V), w("fvu")), ACT.Copy, scale=1.0 / HOME)
+            ts(w("cc"), w("cci"), w("pcol", 4, 5), -4.0, ALU.subtract, ALU.mult)
         quant(w("landq%d" % t, K, K + 128), w("lands%d" % t, K, K + 128), w("xs", 0, 512))
         if t == 0:
             for e in range(4):
-                ts(w("xp%d" % e, 0, V), w("xs", e, 4 * V, 4), 64.0, None, ALU.mult)
+                ts(w("xp%d" % e, HOME, HOME + V), w("xs", e, 4 * V, 4), 64.0, None, ALU.mult)
         if t < ROUNDS - 1:
             spread_u(t + 1)
             fill(w("pw", F - K, F), 0.0)
         if t == 1:
             quant(w("qwy"), w("swy"), w("wyb"))
+        act(w("flb"), by(w("num"), fo), ACT.Copy)
+        act(w("flr%d" % t), by(w("flb"), w("rev")), ACT.Copy)
+        dma("y", "dfl%d" % t, hbm(T.fl[t:t + 1, :]), w("flr%d" % t, 0, K, 1, 0, 1))
         lst = w("lst%d" % t)
         tt(w("gt"), by(w("fvrow"), lst), w("msk"), ALU.mult)
         act(w("gu", 0, K), by(w("fvrow"), lst), ACT.Copy)
@@ -445,31 +474,27 @@ def rank_program(g, core, T, topo):
             ts(w("f4", 6 * e, 6 * e + 6), lst, 4.0, float(e), ALU.mult, ALU.add)
         act(w("x32"), by(w("hs"), w("f4")), ACT.Copy, scale=32.0)
         for m in range(6):
-            ts(w("ne", SEG * m + 16 * m, SEG * m + SEG), w("gu", 16 * m, SEG), w("s1", 16 * m + 15, 16 * m + 16), None,
-               ALU.not_equal)
+            v = w("s1", 16 * m + 15, 16 * m + 16)
+            ts(w("ne", SEG * m + 16 * m, SEG * m + SEG), w("gu", 16 * m, SEG), v, v, ALU.not_equal, ALU.add)
         scan(w("win"), w("cc"), w("ne"), 0.0, ALU.max, ALU.min)
         for b in range(4):
             mm(bank(b, 0, 128), w("qw", 128 * b, 128 * b + 128), w("sw", 128 * b, 128 * b + 128),
                w("landq%d" % t, 0, 128), w("lands%d" % t, 0, 128))
-        ts(w("u1", 0, 6), w("s1", 15, K, 16), 1.0 / SPARE, None, ALU.mult)
-        tt(w("dst", 0, 6), w("u1", 0, 6), w("win", SEG - 1, 6 * SEG, SEG), ALU.subtract)
 
         def blend(b):
             tt(w("zb", K * b, K * b + K), bank(b, 0, K), w("x32", K * b, K * b + K), ALU.add)
 
-        ts(w("ob", 0, 6), w("dst", 0, 6), float(SPARE), float(SPARE - 1), ALU.mult, ALU.add)
+        ts(w("ob", 0, 6), w("win", SEG - 1, 6 * SEG, SEG), float(HOME), None, ALU.mult)
         blend(0)
+        blend(1)
         for b in range(4):
-            if b < 3:
-                blend(b + 1)
             cp(by(w("xp%d" % b), w("ob", 0, 6)), w("zb", K * b, K * b + K))
-        act(w("flb"), by(w("num"), w(fo)), ACT.Copy)
-        act(w("flr%d" % t), by(w("flb"), w("rev")), ACT.Copy)
-        dma("y", "dfl%d" % t, hbm(T.fl[t:t + 1, :]), w("flr%d" % t, 0, K, 1, 0, 1))
+            if b < 2:
+                blend(b + 2)
 
     for e in range(3):
-        act(w("xs", e, 4 * V, 4), w("xp%d" % e, 0, V), ACT.Copy, scale=0.015625)
-    ts(w("xs", 3, 4 * V, 4), w("xp3", 0, V), 0.015625, None, ALU.mult)
+        act(w("xs", e, 4 * V, 4), w("xp%d" % e, HOME, HOME + V), ACT.Copy, scale=0.015625)
+    ts(w("xs", 3, 4 * V, 4), w("xp3", HOME, HOME + V), 0.015625, None, ALU.mult)
     n = V // 2
     for h in range(2):
         quant(w("qx", n * h, n * h + n), w("sx", n * h, n * h + n), w("xs", 4 * n * h, 4 * n * h + 4 * n))

@@ -3,86 +3,40 @@ from concourse.mybir import dt, AluOpType, ActivationFunctionType
 ALU = AluOpType
 ACT = ActivationFunctionType
 V, F, K, ROUNDS = 384, 768, 96, 3
-HOME = 512
+PLANE = 1024
+SPANS = [(256, 384), (0, 256)]
 CODE = "float8_e4m3fn_x4"
 SEG = K + 2
 FW, CW = 768, 384
 STEP = 0.625 * 2.0 ** -23
 TINY = 2.0 ** -120
+DROP = -4096.0
+GA = 192
+N5 = 384
+VB = (3, 4, 5)
 
-SCRATCH = {
-    "ps": ("psum", [128, 4096], "float32"),
-    "fvi": ("sbuf", [128, 48], "int32"),
-    "fvu": ("sbuf", [128, 48], "uint16"),
-    "o4": ("sbuf", [128, 192], "uint16"),
-    "xs": ("sbuf", [128, 4 * V], "bfloat16"),
-    "hs": ("sbuf", [128, 4 * F], "bfloat16"),
-    "ub": ("sbuf", [128, 512], "bfloat16"),
-    "qu": ("sbuf", [128, 128], CODE),
-    "su": ("sbuf", [128, 128], "uint8"),
-    "ubc": ("sbuf", [128, 384], CODE),
-    "sbc": ("sbuf", [128, 384], "uint8"),
-    "uoff": ("sbuf", [128, 24], "uint16"),
-    "wyb": ("sbuf", [128, 512], "bfloat16"),
-    "qwy": ("sbuf", [128, 128], CODE),
-    "swy": ("sbuf", [128, 128], "uint8"),
-    "qw": ("sbuf", [128, 512], CODE),
-    "sw": ("sbuf", [128, 512], "uint8"),
-    "qx": ("sbuf", [128, V], CODE),
-    "sx": ("sbuf", [128, V], "uint8"),
-    "ysb": ("sbuf", [128, V], "float32"),
-    "scol": ("sbuf", [128, 8], "float32"),
-    "gap": ("sbuf", [128, 8], "float32"),
-    "tri": ("sbuf", [128, 128], "bfloat16"),
-    "bar": ("sbuf", [128, F], "float32"),
-    "acc": ("sbuf", [128, 8], "float32"),
-    "acb": ("sbuf", [128, 8], "float32"),
-    "flags": ("sbuf", [128, 6 * FW], "bfloat16"),
-    "sg": ("sbuf", [128, 2304], "bfloat16"),
-    "cnt": ("sbuf", [128, 6 * CW], "float16"),
-    "pos": ("sbuf", [128, 8], "uint16"),
-    "pw": ("sbuf", [128, F + 16], "float32"),
-    "tra": ("sbuf", [128, 96], "float32"),
-    "trc": ("sbuf", [128, 128], "float32"),
-    "u1": ("sbuf", [128, 8], "float32"),
-    "u2": ("sbuf", [128, 8], "float32"),
-    "u3": ("sbuf", [128, 8], "float32"),
-    "num": ("sbuf", [128, F], "float32"),
-    "fvrow": ("sbuf", [128, F], "float32"),
-    "pidx": ("sbuf", [128, 4], "int32"),
-    "pcol": ("sbuf", [128, 8], "float32"),
-    "fid": ("sbuf", [128, K], "float32"),
-    "dif": ("sbuf", [128, K], "float32"),
-    "msk": ("sbuf", [128, K], "float32"),
-    "rst": ("sbuf", [128, K], "float32"),
-    "cci": ("sbuf", [128, 6 * SEG], "bfloat16"),
-    "cc": ("sbuf", [128, 6 * SEG], "float16"),
-    "turn": ("sbuf", [128, 2], "uint16"),
-    "revi": ("sbuf", [128, 6], "float32"),
-    "rev": ("sbuf", [128, 6], "uint16"),
-    "f4": ("sbuf", [128, 24], "uint16"),
-    "ob": ("sbuf", [128, 8], "uint16"),
-    "gt": ("sbuf", [128, K], "float32"),
-    "gu": ("sbuf", [128, SEG + 2], "float32"),
-    "s1": ("sbuf", [128, K], "float32"),
-    "ne": ("sbuf", [128, 6 * SEG], "float16"),
-    "win": ("sbuf", [128, 6 * SEG], "float16"),
-    "x32": ("sbuf", [128, 4 * K], "float32"),
-    "zb": ("sbuf", [128, 4 * K], "bfloat16"),
-    "flb": ("sbuf", [128, K], "float32"),
+_WIDTH = {
+    "int32": {"fvi": 48},
+    "uint16": {"fvu": 48, "o4": 192, "uoff": 24, "cnt": 6 * CW, "turn": 2, "rev": 6, "f4": 24, "win": 6 * SEG},
+    "bfloat16": {"xs": 4 * V, "hs": 4 * F, "ub": 512, "wyb": 512, "tri": 128, "flags": 6 * FW, "sg": 2304, "fvrow": F,
+                 "msk": K, "rst": K, "gt": K, "gu": SEG + 2, "s1": K, "zb": 4 * K},
+    "float16": {"cc": SEG, "ne": 6 * SEG},
+    "float32": {"ysb": V, "scol": 8, "gap": 8, "bar": F, "acc": 8, "pw": F + 16, "tr": 224, "u2": 28, "u3": 16, "far": 96,
+                "num": PLANE, "prow": 128, "pcol": 128, "fid": K, "dif": K, "revi": 6, "x32": 4 * K, "flb": K},
+    CODE: {"qu": 128, "ubc": 384, "qwy": 128, "qw": 512, "qx": V},
+    "uint8": {"su": 128, "sbc": 384, "swy": 128, "sw": 512, "sx": V},
 }
 for _t in range(4):
-    SCRATCH["xp%d" % _t] = ("sbuf", [128, HOME + V], "bfloat16")
+    _WIDTH["bfloat16"]["xp%d" % _t] = PLANE
 for _t in range(ROUNDS):
-    SCRATCH["qh%d" % _t] = ("sbuf", [128, F], CODE)
-    SCRATCH["sh%d" % _t] = ("sbuf", [128, F], "uint8")
-    SCRATCH["fo%d" % _t] = ("sbuf", [128, 16], "uint16")
-    SCRATCH["lst%d" % _t] = ("sbuf", [128, 6], "uint16")
-    SCRATCH["slotq%d" % _t] = ("sbuf", [128, K], CODE)
-    SCRATCH["slots%d" % _t] = ("sbuf", [128, K], "uint8")
-    SCRATCH["landq%d" % _t] = ("sbuf", [128, K + 128], CODE)
-    SCRATCH["lands%d" % _t] = ("sbuf", [128, K + 128], "uint8")
-    SCRATCH["flr%d" % _t] = ("sbuf", [128, K], "float32")
+    _WIDTH[CODE].update({"qh%d" % _t: F, "slotq%d" % _t: K, "landq%d" % _t: K + 128})
+    _WIDTH["uint8"].update({"sh%d" % _t: F, "slots%d" % _t: K, "lands%d" % _t: K + 128})
+    _WIDTH["uint16"].update({"fo%d" % _t: 16, "lst%d" % _t: 6})
+    _WIDTH["float32"]["flr%d" % _t] = K
+SCRATCH = {"ps": ("psum", [128, 4096], "float32")}
+for _d in _WIDTH:
+    for _n in _WIDTH[_d]:
+        SCRATCH[_n] = ("sbuf", [128, _WIDTH[_d][_n]], _d)
 
 SEMAPHORES = ["cv", "cs", "cp", "cg", "sent", "dfv", "dx", "du", "dwc", "dws", "dwy", "dout", "dy"]
 SEMAPHORES += ["list%d" % _t for _t in range(ROUNDS)] + ["data%d" % _t for _t in range(ROUNDS)]
@@ -93,9 +47,7 @@ def _overlap(a, b):
     if a[0] != b[0]:
         return False
     if a[0] == "ps":
-        ba = set(c // 512 for c in range(a[3], a[4], a[5]))
-        bb = set(c // 512 for c in range(b[3], b[4], b[5]))
-        return bool(ba & bb)
+        return a[3] // 512 <= (b[4] - 1) // 512 and b[3] // 512 <= (a[4] - 1) // 512
     if a[2] <= b[1] or b[2] <= a[1] or a[4] <= b[3] or b[4] <= a[3]:
         return False
     if a[5] == b[5] and a[5] > 1 and a[3] % a[5] != b[3] % b[5]:
@@ -133,7 +85,7 @@ def rank_program(g, core, T, topo):
     own = {"v": "cv", "s": "cs", "p": "cp", "g": "cg"}
     total = {}
     known = {q: {} for q in eng}
-    log = []
+    log = {}
 
     def w(name, lo=None, hi=None, step=1, p0=0, p1=128):
         t = T[name]
@@ -163,22 +115,25 @@ def rank_program(g, core, T, topo):
 
     def order(q, reads, writes):
         need = {}
-        for (reg, wr, q0, sem, count, clock) in log:
-            hit = any(_overlap(reg, x) for x in writes)
-            if not hit and (wr or (reg[0] == "ps" and q0 != q)):
-                hit = any(_overlap(reg, x) for x in reads)
-            if hit and known[q].get(sem, 0) < count and need.get(sem, (0,))[0] < count:
-                need[sem] = (count, clock)
-        for sem in sorted(need, key=lambda s: -len(need[s][1])):
+        for name in sorted(set(x[0] for x in reads + writes)):
+            for (reg, wr, q0, sem, count, clock) in log.get(name, []):
+                if known[q].get(sem, 0) >= count or need.get(sem, (0,))[0] >= count:
+                    continue
+                hit = any(_overlap(reg, x) for x in writes)
+                if not hit and (wr or (name == "ps" and q0 != q)):
+                    hit = any(_overlap(reg, x) for x in reads)
+                if hit:
+                    need[sem] = (count, clock)
+        for sem in sorted(need, key=lambda s: (-len(need[s][1]), s)):
             wait(q, sem, need[sem][0], need[sem][1])
 
     def note(q, sem, inc, reads, writes):
         total[sem] = total.get(sem, 0) + inc
         clock = dict(known[q])
         for r in reads:
-            log.append((r, False, q, sem, total[sem], clock))
+            log.setdefault(r[0], []).append((r, False, q, sem, total[sem], clock))
         for r in writes:
-            log.append((r, True, q, sem, total[sem], clock))
+            log.setdefault(r[0], []).append((r, True, q, sem, total[sem], clock))
 
     def op(q, call, out, ins, extra=None):
         reads = [r for a in ins for r in a[1]]
@@ -196,14 +151,14 @@ def rank_program(g, core, T, topo):
     def hbm(ap):
         return (ap, [])
 
-    def ts(out, a, s1, s2, op0, op1=None, q="v"):
+    def ts(out, a, s1, s2, op0, op1=None):
         ins = [a] + [s for s in (s1, s2) if isinstance(s, tuple)]
         x1 = s1[0] if isinstance(s1, tuple) else s1
         x2 = s2[0] if isinstance(s2, tuple) else s2
         if op1 is None:
-            op(q, lambda: g.vector.tensor_scalar(out[0], a[0], x1, None, op0), out, ins)
+            op("v", lambda: g.vector.tensor_scalar(out[0], a[0], x1, None, op0), out, ins)
         else:
-            op(q, lambda: g.vector.tensor_scalar(out[0], a[0], x1, x2, op0, op1), out, ins)
+            op("v", lambda: g.vector.tensor_scalar(out[0], a[0], x1, x2, op0, op1), out, ins)
 
     def tt(out, a, b, o):
         op("v", lambda: g.vector.tensor_tensor(out[0], a[0], b[0], o), out, [a, b])
@@ -240,11 +195,11 @@ def rank_program(g, core, T, topo):
     def mm(out, lq, ls, rq, rs):
         op("p", lambda: g.tensor.matmul_mx(out[0], lq[0], ls[0], rq[0], rs[0], True, True), out, [lq, ls, rq, rs])
 
-    def iota(out, pattern, base, mult, small=True):
-        if small:
-            op("g", lambda: g.iota(out[0], pattern, base, mult, allow_small_or_imprecise_dtypes=True), out, [])
-        else:
-            op("g", lambda: g.iota(out[0], pattern, base, mult), out, [])
+    def iota(out, pattern, base, mult):
+        op("g", lambda: g.iota(out[0], pattern, base, mult, allow_small_or_imprecise_dtypes=True), out, [])
+
+    def row(out, n, p, c):
+        op("g", lambda: g.affine_select(out[0], out[0], [[0, n]], ALU.not_equal, c, -p, 1), out, [out])
 
     def remote(t, sem, dst, src, engines):
         order("g", src[1], [])
@@ -256,9 +211,9 @@ def rank_program(g, core, T, topo):
         a, b = len(theirs[t][0]), len(theirs[t][1])
         total["list%d" % t] = a
         total["data%d" % t] = a + b
-        log.append((w("lst%d" % t)[1][0], True, "far", "list%d" % t, a, {}))
-        log.append((w("landq%d" % t, 0, K)[1][0], True, "far", "data%d" % t, a + b, {}))
-        log.append((w("lands%d" % t, 0, K)[1][0], True, "far", "data%d" % t, a + b, {}))
+        for reg, sem, n in ((w("lst%d" % t), "list%d" % t, a), (w("landq%d" % t, 0, K), "data%d" % t, a + b),
+                            (w("lands%d" % t, 0, K), "data%d" % t, a + b)):
+            log.setdefault(reg[1][0][0], []).append((reg[1][0], True, "far", sem, n, {}))
 
     dma("y", "dfv", w("fvi"), hbm(T.fv[:]))
     dma("y", "dx", w("xs"), hbm(T.x[:]))
@@ -268,40 +223,52 @@ def rank_program(g, core, T, topo):
     dma("y", "dws", w("sw"), hbm(T.ws[:]))
     dma("y", "dwy", w("wyb"), hbm(T.wy[:]))
 
-    iota(w("pidx", 0, 1), [[0, 1]], 0, 1, small=False)
+    place_, first_, which_, own_ = [w("pcol", 32 * i, 32 * i + 1) for i in range(4)]
+    iota(w("prow", 0, 32), [[0, 2], [1, 16]], 0, 0)
+    iota(w("prow", 32, 64), [[16, 2], [0, 16]], 0, 1)
+    iota(w("prow", 64, 80), [[1, 8], [-3, 2]], 4, 0)
+    iota(w("prow", 80, 96), [[1, 8], [4, 2]], 0, 0)
+    iota(w("prow", 96, 128), [[0, 2], [1, 16]], 1, 0)
     iota(w("fid"), [[128, 6], [1, 16]], 0, 0)
-    iota(w("dif"), [[0, 6], [1, 16]], 0, 0)
-    iota(w("revi"), [[-16, 6]], K - 1, 0)
     fill(w("tri"), 1.0)
-    op("g", lambda: g.affine_select(T.tri[:], T.tri[:], [[1, 128]], ALU.is_gt, 0.0, 0, -1), w("tri"), [w("tri")])
-    iota(w("num"), [[1, F]], 0, 0)
-    iota(w("cci"), [[-16, 6], [1, SEG]], 0, 0)
+    fill(w("pw", F - K - 16, F + 16), 0.0)
     for t in range(ROUNDS):
         fill(w("uoff", 8 * t, 8 * t + 8), t)
-    fill(w("pw", F - K - 16, F + 16), 0.0)
     fill(w("rst"), 1.0)
-    fill(w("ne"), 0.0)
     fill(w("gu", K, SEG + 2), -1.0)
     fill(w("u3"), 0.0)
     fill(w("rst", 0, K, 16), 0.0)
-    ts(w("pidx", 1, 2), w("pidx", 0, 1), 15, None, ALU.bitwise_and)
-    ts(w("pidx", 2, 3), w("pidx", 0, 1), 112, None, ALU.bitwise_and)
-    ts(w("pidx", 3, 4), w("pidx", 0, 1), 16, None, ALU.bitwise_and)
-    cp(w("pcol", 0, 3), w("pidx", 1, 4))
-    ts(w("fid"), w("fid"), w("pcol", 1, 2), None, ALU.add)
-    ts(w("msk"), w("dif"), w("pcol", 0, 1), None, ALU.is_equal)
-    ts(w("rev"), w("revi"), w("pcol", 0, 1), None, ALU.subtract)
-    ts(w("pcol", 3, 4), w("pcol", 2, 3), -0.0625, 1.0, ALU.mult, ALU.add)
-    ts(w("pcol", 4, 5), w("pcol", 0, 1), 1.5, None, ALU.add)
-    ts(w("turn", 0, 1), w("pcol", 3, 4), w("pcol", 0, 1), 7.0, ALU.add, ALU.min)
-    for e in (1, 2, 3, 0):
+    for e in (1, 0, 3, 2):
         ts(w("o4", 48 * e, 48 * e + 48), w("fvi"), 4.0, float(e), ALU.mult, ALU.add)
-    cp(w("fvu"), w("fvi"))
+    ts(w("far", 0, 48), w("fvi"), 256.0, 0.0, ALU.subtract, ALU.max)
+    turn(w("pcol"), w("prow"))
+    tt(w("far", 48, 96), w("far", 0, 48), w("fvi"), ALU.add)
+    cp(w("turn", 0, 1), which_)
+    ts(w("fvu"), w("far", 48, 96), 2.0, 1.0, ALU.mult, ALU.add)
+    act(w("fid"), w("fid"), ACT.Identity, bias=first_)
+    op("g", lambda: g.affine_select(T.tri[:], T.tri[:], [[1, 128]], ALU.is_gt, 0.0, 0, -1), w("tri"), [w("tri")])
+    for p in (88, 120):
+        row(w("pw", F - K - 16, F + 16), 128, p, DROP)
+    for p, c in ((72, 0.0), (88, DROP), (104, 0.0), (120, DROP)):
+        row(w("fid"), K, p, c)
+    iota(w("num"), [[1, PLANE]], 0, 0)
+    iota(w("dif"), [[0, 6], [1, 16]], 0, 0)
+    iota(w("revi"), [[-16, 6]], K - 1, 0)
+
+    def home(e, lo, hi):
+        if hi <= 256:
+            return w("xp%d" % e, 2 * lo + 1, 2 * hi, 2)
+        return w("xp%d" % e, 4 * lo - 511, 4 * hi - 512, 4)
 
     def spread_u(a):
         off = w("uoff", 8 * a, 8 * a + 8)
         cp(words(w("ubc", 128 * a, 128 * a + 128)), by(words(w("qu")), off))
         act(w("sbc", 128 * a, 128 * a + 128), by(w("su"), off), ACT.Copy)
+
+    def fired(t):
+        act(w("flb"), by(w("num"), w("fo%d" % t, 0, 6)), ACT.Copy)
+        act(w("flr%d" % t), by(w("flb"), w("rev")), ACT.Copy)
+        dma("y", "dfl%d" % t, hbm(T.fl[t:t + 1, :]), w("flr%d" % t, 0, K, 1, 0, 1))
 
     def bank(b, lo=0, hi=V):
         return w("ps", 512 * b + lo, 512 * b + hi)
@@ -310,16 +277,16 @@ def rank_program(g, core, T, topo):
         qh, sh = "qh%d" % t, "sh%d" % t
         uq, us = w("ubc", 128 * t, 128 * t + 128), w("sbc", 128 * t, 128 * t + 128)
 
-        def gather(q, e, h):
-            out = w("hs", 4 * V * h + e, 4 * V * h + 4 * V, 4)
+        def gather(q, e, lo, hi):
+            out = w("hs", 4 * lo + e, 4 * hi, 4)
             if t == 0:
-                src = by(w("xs"), w("o4", 48 * e + 24 * h, 48 * e + 24 * h + 24))
+                src = by(w("xs"), w("o4", 48 * e + lo // 16, 48 * e + hi // 16))
                 if q == "v":
                     cp(out, src)
                 else:
                     act(out, src, ACT.Copy)
             else:
-                src = by(w("xp%d" % e, HOME, HOME + V), w("fvu", 24 * h, 24 * h + 24))
+                src = by(w("xp%d" % e), w("fvu", lo // 16, hi // 16))
                 if q == "v":
                     ts(out, src, 0.015625, None, ALU.mult)
                 else:
@@ -327,31 +294,38 @@ def rank_program(g, core, T, topo):
 
         def half(h):
             quant(w(qh, V * h, V * h + V), w(sh, V * h, V * h + V), w("hs", 4 * V * h, 4 * V * h + 4 * V))
-            for c in range(3 * h, 3 * h + 3):
-                mm(bank(c % 3, 0, 128), w(qh, 128 * c, 128 * c + 128), w(sh, 128 * c, 128 * c + 128), uq, us)
-            for b in ((3, 4), (6, 5))[h]:
-                mm(bank(b), uq, us, w(qh, V * h, V * h + V), w(sh, V * h, V * h + V))
+            cols = [(bank(c % 3, 0, 128), w(qh, 128 * c, 128 * c + 128), w(sh, 128 * c, 128 * c + 128), uq, us)
+                    for c in range(3 * h, 3 * h + 3)]
+            rows = [(bank(b), uq, us, w(qh, V * h, V * h + V), w(sh, V * h, V * h + V)) for b in ((3, 4), (5,))[h]]
+            for a in (rows + cols if h else cols + rows):
+                mm(*a)
 
         def col(c):
             return w("scol", c, c + 1)
 
         lt, le = ALU.is_lt, ALU.is_le
-        mine_v = {0: [(0, 128, 384, le)], 1: [(0, 0, 128, lt), (0, 256, 384, le)], 2: [],
-                  3: [(0, 0, 384, lt), (1, 128, 384, le)],
-                  4: [(0, 0, 384, lt), (1, 0, 128, lt), (1, 256, 384, le)],
-                  5: [(0, 0, 384, lt), (1, 0, 256, lt)]}
-        early = [(2, 0, 0, 256, False, "acc")]
-        late = [(0, 1, 0, 384, True, "acb"), (1, 1, 0, 384, True, "acb"), (2, 1, 0, 384, True, "acb")]
+        mine_v = {0: [(1, 0, 384, le)], 1: [(0, 0, 128, lt), (0, 256, 384, le), (1, 0, 384, le)],
+                  2: [(1, 0, 384, le)], 3: [(1, 128, 384, le)],
+                  4: [(1, 0, 128, lt), (1, 256, 384, le)],
+                  5: [(0, N5, 384, lt), (1, 0, 256, lt)]}
+        early = [(2, 0, 256, False), (0, 128, 384, True)]
+        late = [(5, 0, N5, False), (4, 0, 384, False), (3, 0, 384, False)]
         place = {}
         at = 0
         for j in early + late:
             place[j] = at
-            at += j[3] - j[2]
+            at += j[2] - j[1]
 
-        def bars(h, src):
-            act(w("gap", 3 * h, 3 * h + 3), src, ACT.Abs, bias=TINY, scale=STEP)
-            for c in range(3 * h, 3 * h + 3):
-                act(w("bar", 128 * c, 128 * c + 128), w("tri"), ACT.Identity, bias=col(c), scale=w("gap", c, c + 1))
+        def scores(h):
+            act(w("scol", 3 * h, 3 * h + 3), w("ps", 0, 1536, 512), ACT.Copy)
+            act(w("gap", 3 * h, 3 * h + 3), w("ps", 0, 1536, 512), ACT.Abs, bias=TINY, scale=STEP)
+
+        def bar(c):
+            out = w("bar", 128 * c, 128 * c + 128)
+            if c in VB:
+                ts(out, w("tri"), w("gap", c, c + 1), col(c), ALU.mult, ALU.add)
+            else:
+                act(out, w("tri"), ACT.Identity, bias=col(c), scale=w("gap", c, c + 1))
 
         def block(c):
             d = 128 * (c % 3)
@@ -360,89 +334,94 @@ def rank_program(g, core, T, topo):
         def compare(c, which):
             a = FW * c + 128
             for i, (h, lo, hi, o) in enumerate(mine_v[c]):
-                if i in which:
+                if i in which and hi > lo:
                     ts(w("flags", a, a + hi - lo), bank(3 + 2 * h, lo, hi), col(c), None, o)
                 a += hi - lo
 
         def count(c):
             n = (128 + sum(j[2] - j[1] for j in mine_v[c])) // 2
-            init = w("acc", c, c + 1) if any(j[0] == c for j in early) else 0.0
-            scan(w("cnt", CW * c + CW - n, CW * c + CW), w("flags", FW * c, FW * c + n),
+            init = w("acc", c, c + 1) if any(j[0] == c for j in early + late) else 0.0
+            scan(w("cnt", 6 * (CW - n) + c, 6 * CW, 6), w("flags", FW * c, FW * c + n),
                  w("flags", FW * c + n, FW * c + 2 * n), init, ALU.add, ALU.add)
 
         def sign1(j):
-            act(w("sg", place[j], place[j] + j[3] - j[2]), bank(4 + 2 * j[1], j[2], j[3]), ACT.Sign, bias=col(j[0]), scale=-1.0)
+            act(w("sg", place[j], place[j] + j[2] - j[1]), bank(4, j[1], j[2]), ACT.Sign, bias=col(j[0]), scale=-1.0)
 
         def sign2(j):
-            a = w("sg", place[j], place[j] + j[3] - j[2])
-            if j[4]:
-                act(a, a, ACT.Sign, bias=1.0, accum=w(j[5], j[0], j[0] + 1))
+            a = w("sg", place[j], place[j] + j[2] - j[1])
+            if j[3]:
+                act(a, a, ACT.Sign, bias=1.0, accum=w("acc", j[0], j[0] + 1))
             else:
-                act(a, a, ACT.Relu, accum=w(j[5], j[0], j[0] + 1))
-
-        def spot(c):
-            ts(w("pos", c, c + 1), w("cnt", CW * c + CW - 1, CW * c + CW), w("acb", c, c + 1), None, ALU.add)
+                act(a, a, ACT.Relu, accum=w("acc", j[0], j[0] + 1))
 
         if t == 0:
-            gather("s", 1, 0)
-            gather("v", 0, 0)
-            gather("s", 2, 0)
+            gather("s", 1, 0, V)
+            gather("v", 0, 0, V)
+            gather("s", 3, 0, V)
             quant(w("qu"), w("su"), w("ub"))
-            gather("v", 3, 0)
+            gather("v", 2, 0, V)
             spread_u(0)
         else:
-            for e in range(3):
-                gather("s", e, 0)
-            gather("v", 3, 0)
-        gather("s", 0, 1)
-        gather("s", 1, 1)
+            gather("s", 0, 0, V)
+            gather("s", 1, 0, V)
+            gather("v", 2, 0, V)
+            gather("s", 3, 0, V)
+            gather("v", 3, V, V + GA)
+        gather("s", 0, V, F)
+        gather("s", 1, V, F)
         half(0)
-        gather("v", 3, 1)
-        gather("s", 2, 1)
-        cp(w("scol", 0, 3), w("ps", 0, 1536, 512))
-        bars(0, w("scol", 0, 3))
-        compare(0, [0])
-        compare(1, [0, 1])
+        gather("v", 2, V, F)
+        scores(0)
+        gather("v", 3, V + GA if t else V, F)
+        for c in range(3):
+            bar(c)
+        compare(1, [0])
         half(1)
-        for j in early:
-            sign1(j)
-        for j in early:
-            sign2(j)
-        act(w("scol", 3, 6), w("ps", 0, 1536, 512), ACT.Copy)
-        bars(1, w("ps", 0, 1536, 512))
+        compare(1, [1])
+        sign1(early[0])
+        sign1(early[1])
+        sign2(early[0])
+        sign2(early[1])
         for c in range(3):
             block(c)
-        for c in range(3):
-            count(c)
+        scores(1)
         sign1(late[0])
+        for c in range(3, 6):
+            if c not in VB:
+                bar(c)
         sign1(late[1])
         sign2(late[0])
         sign1(late[2])
         sign2(late[1])
         sign2(late[2])
+        compare(1, [2])
+        compare(0, [0])
+        count(1)
+        compare(2, [0])
         for c in range(3, 6):
-            compare(c, [0])
-        for c in range(3, 6):
+            if c in VB:
+                bar(c)
+        count(0)
+        compare(5, [0, 1])
+        count(2)
+        for c in (5, 4, 3):
             block(c)
-        compare(3, [1])
-        compare(4, [1, 2])
-        count(3)
-        compare(5, [1])
-        count(4)
-        spot(0)
+        compare(4, [0, 1])
+        compare(3, [0])
         count(5)
-        spot(1)
-        spot(2)
+        count(4)
+        count(3)
         fo = w("fo%d" % t, 0, 6)
-        cp(w("pos", 3, 6), w("cnt", 4 * CW - 1, 6 * CW, CW))
-        cp(by(w("pw"), w("pos", 0, 6)), w("fid"))
-        turn(w("trc"), w("pw", F - K - 16, F + 16))
-        turn(w("tra"), w("pw", F - K, F))
-        tt(w("u1", 0, 7, 2), w("trc", 0, 128, 32), w("trc", 16, 128, 32), ALU.add)
-        tt(w("u1", 1, 7, 2), w("tra", 0, 96, 32), w("tra", 16, 96, 32), ALU.add)
-        tt(w("u2", 0, 7, 1, 0, 64), w("u1", 0, 7, 1, 0, 64), w("u1", 0, 7, 1, 64, 128), ALU.add)
+        if t == 0:
+            act(w("fvrow"), by(w("num"), w("fvu")), ACT.Identity, bias=-1.0)
+        else:
+            fired(t - 1)
+        cp(by(w("pw"), w("cnt", 6 * CW - 6, 6 * CW)), w("fid"))
+        turn(w("tr", 0, 128), w("pw", F - K - 16, F + 16))
+        turn(w("tr", 128, 224), w("pw", F - K, F))
+        scan(w("u2", 0, 28, 1, 0, 64), w("tr", 0, 224, 8, 0, 64), w("tr", 0, 224, 8, 64, 128), 0.0, ALU.max, ALU.add)
         for a in (0, 32, 64, 96):
-            tt(w("u3", 0, 7, 1, a, a + 32), w("u2", 0, 7, 1, 0, 32), w("u2", 0, 7, 1, 32, 64), ALU.add)
+            tt(w("u3", 0, 7, 1, a, a + 32), w("u2", 2, 28, 4, 0, 32), w("u2", 2, 28, 4, 32, 64), ALU.add)
         cp(w("fo%d" % t), by(w("u3"), w("turn", 0, 1)))
         remote(t, "list%d" % t, w("lst%d" % t), fo, mine[t][0])
         cp(words(w("slotq%d" % t)), by(words(w(qh)), fo))
@@ -450,63 +429,71 @@ def rank_program(g, core, T, topo):
         remote(t, "data%d" % t, octets(w("landq%d" % t, 0, K)), octets(w("slotq%d" % t)), mine[t][1])
         remote(t, "data%d" % t, w("lands%d" % t, 0, K), w("slots%d" % t), mine[t][0])
         if t == 0:
-            act(w("fvrow"), by(w("num", 0, V), w("fvu")), ACT.Copy, scale=1.0 / HOME)
-            ts(w("cc"), w("cci"), w("pcol", 4, 5), -4.0, ALU.subtract, ALU.mult)
+            ts(w("msk"), w("dif"), place_, None, ALU.is_equal)
+            ts(w("rev"), w("revi"), place_, None, ALU.subtract)
+            ts(w("cc"), w("num", 0, SEG), own_, 2048.0, ALU.is_le, ALU.mult)
         quant(w("landq%d" % t, K, K + 128), w("lands%d" % t, K, K + 128), w("xs", 0, 512))
         if t == 0:
             for e in range(4):
-                ts(w("xp%d" % e, HOME, HOME + V), w("xs", e, 4 * V, 4), 64.0, None, ALU.mult)
+                for lo, hi in SPANS:
+                    ts(home(e, lo, hi), w("xs", 4 * lo + e, 4 * hi, 4), 64.0, None, ALU.mult)
         if t < ROUNDS - 1:
             spread_u(t + 1)
-            fill(w("pw", F - K, F), 0.0)
+            ts(w("pw", F - K, F), w("num", 0, K), 0.0, w("pw", F + 15, F + 16), ALU.mult, ALU.add)
         if t == 1:
             quant(w("qwy"), w("swy"), w("wyb"))
-        act(w("flb"), by(w("num"), fo), ACT.Copy)
-        act(w("flr%d" % t), by(w("flb"), w("rev")), ACT.Copy)
-        dma("y", "dfl%d" % t, hbm(T.fl[t:t + 1, :]), w("flr%d" % t, 0, K, 1, 0, 1))
+        if t == ROUNDS - 1:
+            fired(t)
         lst = w("lst%d" % t)
-        tt(w("gt"), by(w("fvrow"), lst), w("msk"), ALU.mult)
-        act(w("gu", 0, K), by(w("fvrow"), lst), ACT.Copy)
-        for e in range(2):
-            ts(w("f4", 6 * e, 6 * e + 6), lst, 4.0, float(e), ALU.mult, ALU.add)
-        scan(w("s1"), w("rst"), w("gt"), 0.0, ALU.mult, ALU.add)
-        for e in range(2, 4):
-            ts(w("f4", 6 * e, 6 * e + 6), lst, 4.0, float(e), ALU.mult, ALU.add)
-        act(w("x32"), by(w("hs"), w("f4")), ACT.Copy, scale=32.0)
-        for m in range(6):
-            v = w("s1", 16 * m + 15, 16 * m + 16)
-            ts(w("ne", SEG * m + 16 * m, SEG * m + SEG), w("gu", 16 * m, SEG), v, v, ALU.not_equal, ALU.add)
-        scan(w("win"), w("cc"), w("ne"), 0.0, ALU.max, ALU.min)
-        for b in range(4):
-            mm(bank(b, 0, 128), w("qw", 128 * b, 128 * b + 128), w("sw", 128 * b, 128 * b + 128),
-               w("landq%d" % t, 0, 128), w("lands%d" % t, 0, 128))
+
+        def old(e):
+            for x in (e, e + 1):
+                ts(w("f4", 6 * x, 6 * x + 6), lst, 4.0, float(x), ALU.mult, ALU.add)
+            act(w("x32", K * e, K * e + 2 * K), by(w("hs"), w("f4", 6 * e, 6 * e + 12)), ACT.Copy, scale=32.0)
 
         def blend(b):
             tt(w("zb", K * b, K * b + K), bank(b, 0, K), w("x32", K * b, K * b + K), ALU.add)
 
-        ts(w("ob", 0, 6), w("win", SEG - 1, 6 * SEG, SEG), float(HOME), None, ALU.mult)
+        tt(w("gt"), by(w("fvrow"), lst), w("msk"), ALU.mult)
+        act(w("gu", 0, K), by(w("fvrow"), lst), ACT.Copy)
+        old(0)
+        scan(w("s1"), w("rst"), w("gt"), 0.0, ALU.mult, ALU.add)
+        old(2)
+        for m in range(6):
+            v = w("s1", 16 * m + 15, 16 * m + 16)
+            ts(w("ne", SEG * m, SEG * m + SEG - 16 * m), w("gu", 16 * m, SEG), v, v, ALU.not_equal, ALU.add)
+        for m in range(6):
+            n = SEG - 16 * m
+            scan(w("win", 96 * m + m, 6 * SEG, 6), w("cc", 0, n), w("ne", SEG * m, SEG * m + n), 0.0, ALU.max, ALU.min)
+        for b in range(4):
+            mm(bank(b, 0, 128), w("qw", 128 * b, 128 * b + 128), w("sw", 128 * b, 128 * b + 128),
+               w("landq%d" % t, 0, 128), w("lands%d" % t, 0, 128))
         blend(0)
         blend(1)
         for b in range(4):
-            cp(by(w("xp%d" % b), w("ob", 0, 6)), w("zb", K * b, K * b + K))
+            cp(by(w("xp%d" % b), w("win", 6 * SEG - 6, 6 * SEG)), w("zb", K * b, K * b + K))
             if b < 2:
                 blend(b + 2)
 
     for e in range(3):
-        act(w("xs", e, 4 * V, 4), w("xp%d" % e, HOME, HOME + V), ACT.Copy, scale=0.015625)
-    ts(w("xs", 3, 4 * V, 4), w("xp3", HOME, HOME + V), 0.015625, None, ALU.mult)
-    n = V // 2
-    for h in range(2):
-        quant(w("qx", n * h, n * h + n), w("sx", n * h, n * h + n), w("xs", 4 * n * h, 4 * n * h + 4 * n))
-        mm(bank(4 + h, 0, n), w("qwy"), w("swy"), w("qx", n * h, n * h + n), w("sx", n * h, n * h + n))
-        dma("y", "dout", hbm(T.oc[:, 4 * n * h:4 * n * h + 4 * n]), octets(w("qx", n * h, n * h + n)))
-    act(w("ysb", 0, n), bank(4, 0, n), ACT.Copy)
-    cp(w("ysb", n, V), bank(5, 0, n))
-    for h in range(2):
-        dma("s", "dy", hbm(T.y[:, n * h:n * h + n]), w("ysb", n * h, n * h + n))
+        for lo, hi in SPANS:
+            act(w("xs", 4 * lo + e, 4 * hi, 4), home(e, lo, hi), ACT.Copy, scale=0.015625)
+    for lo, hi in SPANS:
+        ts(w("xs", 4 * lo + 3, 4 * hi, 4), home(3, lo, hi), 0.015625, None, ALU.mult)
+    for i, lo in enumerate((256, 0, 128)):
+        hi = lo + 128
+        quant(w("qx", lo, hi), w("sx", lo, hi), w("xs", 4 * lo, 4 * hi))
+        mm(bank(4 + i, 0, 128), w("qwy"), w("swy"), w("qx", lo, hi), w("sx", lo, hi))
+        if i == 0:
+            dma("y", "dout", hbm(T.oc[:, 4 * lo:4 * hi]), octets(w("qx", lo, hi)))
+    dma("y", "dout", hbm(T.oc[:, 0:1024]), octets(w("qx", 0, 256)))
+    act(w("ysb", 256, 384), bank(4, 0, 128), ACT.Copy)
+    cp(w("ysb", 0, 128), bank(5, 0, 128))
+    cp(w("ysb", 128, 256), bank(6, 0, 128))
+    dma("s", "dy", hbm(T.y[:]), w("ysb"))
     for k in range(4):
         dma("y", "dout", hbm(T.osc[4 * k:4 * k + 4, :]), w("sx", 0, V, 1, 32 * k, 32 * k + 4))
-    last = ["cp", "cs", "cv", "dout", "dy"]
-    for sem in [s for s in SEMAPHORES if s not in last] + last:
+    tail = ["cp", "cs", "cv", "dout", "dy"]
+    for sem in [s for s in SEMAPHORES if s not in tail] + tail:
         if total.get(sem, 0):
             g.wait_ge(T.sem[sem], total[sem])

from concourse.mybir import dt, AluOpType, ActivationFunctionType

ALU = AluOpType
ACT = ActivationFunctionType
V, F, K, ROUNDS = 384, 768, 96, 3
PLANE = 1024
SPANS = [(256, 384), (0, 256)]
CODE = "float8_e4m3fn_x4"
SEG = K + 2
FW, CW = 768, 384
STEP = 0.625 * 2.0 ** -23
TINY = 2.0 ** -120
DROP = -4096.0
GA = 192
N5 = 384
VB = (3, 4, 5)

_WIDTH = {
    "int32": {"fvi": 48},
    "uint16": {"fvu": 48, "o4": 192, "uoff": 24, "cnt": 6 * CW, "turn": 2, "rev": 6, "f4": 24, "win": 6 * SEG},
    "bfloat16": {"xs": 4 * V, "hs": 4 * F, "ub": 512, "wyb": 512, "tri": 128, "flags": 6 * FW, "sg": 2304, "fvrow": F,
                 "msk": K, "rst": K, "gt": K, "gu": SEG + 2, "s1": K, "zb": 4 * K},
    "float16": {"cc": SEG, "ne": 6 * SEG},
    "float32": {"ysb": V, "scol": 8, "gap": 8, "bar": F, "acc": 8, "pw": F + 16, "tr": 224, "u2": 28, "u3": 16, "far": 96,
                "num": PLANE, "prow": 128, "pcol": 128, "fid": K, "dif": K, "revi": 6, "x32": 4 * K, "flb": K},
    CODE: {"qu": 128, "ubc": 384, "qwy": 128, "qw": 512, "qx": V},
    "uint8": {"su": 128, "sbc": 384, "swy": 128, "sw": 512, "sx": V},
}
for _t in range(4):
    _WIDTH["bfloat16"]["xp%d" % _t] = PLANE
for _t in range(ROUNDS):
    _WIDTH[CODE].update({"qh%d" % _t: F, "slotq%d" % _t: K, "landq%d" % _t: K + 128})
    _WIDTH["uint8"].update({"sh%d" % _t: F, "slots%d" % _t: K, "lands%d" % _t: K + 128})
    _WIDTH["uint16"].update({"fo%d" % _t: 16, "lst%d" % _t: 6})
    _WIDTH["float32"]["flr%d" % _t] = K
SCRATCH = {"ps": ("psum", [128, 4096], "float32")}
for _d in _WIDTH:
    for _n in _WIDTH[_d]:
        SCRATCH[_n] = ("sbuf", [128, _WIDTH[_d][_n]], _d)

SEMAPHORES = ["cv", "cs", "cp", "cg", "sent", "dfv", "dx", "du", "dwc", "dws", "dwy", "dout", "dy"]
SEMAPHORES += ["list%d" % _t for _t in range(ROUNDS)] + ["data%d" % _t for _t in range(ROUNDS)]
SEMAPHORES += ["dfl%d" % _t for _t in range(ROUNDS)]


def _overlap(a, b):
    if a[0] != b[0]:
        return False
    if a[0] == "ps":
        return a[3] // 512 <= (b[4] - 1) // 512 and b[3] // 512 <= (a[4] - 1) // 512
    if a[2] <= b[1] or b[2] <= a[1] or a[4] <= b[3] or b[4] <= a[3]:
        return False
    if a[5] == b[5] and a[5] > 1 and a[3] % a[5] != b[3] % b[5]:
        return False
    return True


def _mask(engines):
    m = 0
    for e in engines:
        m |= 1 << e
    return m


def rank_program(g, core, T, topo):
    rank = T.rank_of(core)
    if rank is None:
        return
    partners = [T.cores[rank ^ (1 << t)] for t in range(ROUNDS)]

    def lanes(src):
        r = T.rank_of(src)
        eng = [topo.engines(src, T.cores[r ^ (1 << t)]) for t in range(ROUNDS)]
        common = [e for e in eng[0] if all(e in x for x in eng)]
        out = []
        for x in eng:
            more = [e for e in x if e not in common]
            out.append((common, more if len(more) == len(common) else common))
        return out

    mine = lanes(core)
    theirs = [lanes(partners[t])[t] for t in range(ROUNDS)]

    eng = {"v": g.vector, "s": g.scalar, "p": g.tensor, "g": g, "y": g.sync}
    own = {"v": "cv", "s": "cs", "p": "cp", "g": "cg"}
    total = {}
    known = {q: {} for q in eng}
    log = {}

    def w(name, lo=None, hi=None, step=1, p0=0, p1=128):
        t = T[name]
        if lo is None:
            lo, hi = 0, t.shape[1]
        cols = slice(lo, hi) if step == 1 else slice(lo, hi, step)
        ap = t[:, cols] if (p0, p1) == (0, 128) else t[p0:p1, cols]
        return (ap, [(name, p0, p1, lo, hi, step)])

    def words(a):
        return (a[0].bitcast(dt.uint32), a[1])

    def octets(a):
        return (a[0].bitcast(dt.uint8), a[1])

    def by(win, off):
        return (win[0].indirect(off[0]), win[1] + off[1])

    def wait(q, sem, count, clock):
        k = known[q]
        if k.get(sem, 0) < count:
            eng[q].wait_ge(T.sem[sem], count)
            k[sem] = count
        for s, c in clock.items():
            if k.get(s, 0) < c:
                k[s] = c

    def order(q, reads, writes):
        need = {}
        for name in sorted(set(x[0] for x in reads + writes)):
            for (reg, wr, q0, sem, count, clock) in log.get(name, []):
                if known[q].get(sem, 0) >= count or need.get(sem, (0,))[0] >= count:
                    continue
                hit = any(_overlap(reg, x) for x in writes)
                if not hit and (wr or (name == "ps" and q0 != q)):
                    hit = any(_overlap(reg, x) for x in reads)
                if hit:
                    need[sem] = (count, clock)
        for sem in sorted(need, key=lambda s: (-len(need[s][1]), s)):
            wait(q, sem, need[sem][0], need[sem][1])

    def note(q, sem, inc, reads, writes):
        total[sem] = total.get(sem, 0) + inc
        clock = dict(known[q])
        for r in reads:
            log.setdefault(r[0], []).append((r, False, q, sem, total[sem], clock))
        for r in writes:
            log.setdefault(r[0], []).append((r, True, q, sem, total[sem], clock))

    def op(q, call, out, ins, extra=None):
        reads = [r for a in ins for r in a[1]]
        writes = list(out[1][:1]) + (list(extra[1]) if extra else [])
        reads += out[1][1:]
        order(q, reads, writes)
        call().then_inc(T.sem[own[q]], 1)
        note(q, own[q], 1, reads, writes)

    def dma(q, sem, out, in_):
        order(q, in_[1], out[1])
        eng[q].dma_start(out[0], in_[0]).then_inc(T.sem[sem], 16)
        note(q, sem, 16, in_[1], out[1])

    def hbm(ap):
        return (ap, [])

    def ts(out, a, s1, s2, op0, op1=None):
        ins = [a] + [s for s in (s1, s2) if isinstance(s, tuple)]
        x1 = s1[0] if isinstance(s1, tuple) else s1
        x2 = s2[0] if isinstance(s2, tuple) else s2
        if op1 is None:
            op("v", lambda: g.vector.tensor_scalar(out[0], a[0], x1, None, op0), out, ins)
        else:
            op("v", lambda: g.vector.tensor_scalar(out[0], a[0], x1, x2, op0, op1), out, ins)

    def tt(out, a, b, o):
        op("v", lambda: g.vector.tensor_tensor(out[0], a[0], b[0], o), out, [a, b])

    def cp(out, a):
        op("v", lambda: g.vector.tensor_copy(out[0], a[0]), out, [a])

    def fill(out, c):
        op("v", lambda: g.vector.memset(out[0], c), out, [])

    def turn(out, a):
        op("v", lambda: g.vector.transpose(out[0], a[0]), out, [a])

    def scan(out, a, b, init, op0, op1):
        ins = [a, b] + ([init] if isinstance(init, tuple) else [])
        x = init[0] if isinstance(init, tuple) else init
        op("v", lambda: g.vector.tensor_tensor_scan(out[0], a[0], b[0], x, op0, op1), out, ins)

    def quant(codes, scales, a):
        op("v", lambda: g.vector.quantize_mx(codes[0], scales[0], a[0]), codes, [a], scales)

    def act(out, a, func, bias=None, scale=None, accum=None):
        kw = {}
        ins = [a]
        for name, x in (("bias", bias), ("scale", scale)):
            if x is not None:
                kw[name] = x[0] if isinstance(x, tuple) else x
                if isinstance(x, tuple):
                    ins.append(x)
        if accum is not None:
            kw["accum_out"] = accum[0]
        op("s", lambda: g.scalar.activation(out[0], a[0], func, **kw), out, ins, accum)

    def mm(out, lq, ls, rq, rs):
        op("p", lambda: g.tensor.matmul_mx(out[0], lq[0], ls[0], rq[0], rs[0], True, True), out, [lq, ls, rq, rs])

    def iota(out, pattern, base, mult):
        op("g", lambda: g.iota(out[0], pattern, base, mult, allow_small_or_imprecise_dtypes=True), out, [])

    def row(out, n, p, c):
        op("g", lambda: g.affine_select(out[0], out[0], [[0, n]], ALU.not_equal, c, -p, 1), out, [out])

    def remote(t, sem, dst, src, engines):
        order("g", src[1], [])
        rid, pid = topo.addr(partners[t], core)
        g.remote_dma(dst[0], src[0], T.sem[sem], T.sem["sent"], pid, rid, _mask(engines))
        total["sent"] = total.get("sent", 0) + len(engines)

    for t in range(ROUNDS):
        a, b = len(theirs[t][0]), len(theirs[t][1])
        total["list%d" % t] = a
        total["data%d" % t] = a + b
        for reg, sem, n in ((w("lst%d" % t), "list%d" % t, a), (w("landq%d" % t, 0, K), "data%d" % t, a + b),
                            (w("lands%d" % t, 0, K), "data%d" % t, a + b)):
            log.setdefault(reg[1][0][0], []).append((reg[1][0], True, "far", sem, n, {}))

    dma("y", "dfv", w("fvi"), hbm(T.fv[:]))
    dma("y", "dx", w("xs"), hbm(T.x[:]))
    dma("y", "du", w("ub"), hbm(T.u[:]))
    wait("y", "du", 16, {})
    dma("y", "dwc", octets(w("qw")), hbm(T.wc[:]))
    dma("y", "dws", w("sw"), hbm(T.ws[:]))
    dma("y", "dwy", w("wyb"), hbm(T.wy[:]))

    place_, first_, which_, own_ = [w("pcol", 32 * i, 32 * i + 1) for i in range(4)]
    iota(w("prow", 0, 32), [[0, 2], [1, 16]], 0, 0)
    iota(w("prow", 32, 64), [[16, 2], [0, 16]], 0, 1)
    iota(w("prow", 64, 80), [[1, 8], [-3, 2]], 4, 0)
    iota(w("prow", 80, 96), [[1, 8], [4, 2]], 0, 0)
    iota(w("prow", 96, 128), [[0, 2], [1, 16]], 1, 0)
    iota(w("fid"), [[128, 6], [1, 16]], 0, 0)
    fill(w("tri"), 1.0)
    fill(w("pw", F - K - 16, F + 16), 0.0)
    for t in range(ROUNDS):
        fill(w("uoff", 8 * t, 8 * t + 8), t)
    fill(w("rst"), 1.0)
    fill(w("gu", K, SEG + 2), -1.0)
    fill(w("u3"), 0.0)
    fill(w("rst", 0, K, 16), 0.0)
    for e in (1, 0, 3, 2):
        ts(w("o4", 48 * e, 48 * e + 48), w("fvi"), 4.0, float(e), ALU.mult, ALU.add)
    ts(w("far", 0, 48), w("fvi"), 256.0, 0.0, ALU.subtract, ALU.max)
    turn(w("pcol"), w("prow"))
    tt(w("far", 48, 96), w("far", 0, 48), w("fvi"), ALU.add)
    cp(w("turn", 0, 1), which_)
    ts(w("fvu"), w("far", 48, 96), 2.0, 1.0, ALU.mult, ALU.add)
    act(w("fid"), w("fid"), ACT.Identity, bias=first_)
    op("g", lambda: g.affine_select(T.tri[:], T.tri[:], [[1, 128]], ALU.is_gt, 0.0, 0, -1), w("tri"), [w("tri")])
    for p in (88, 120):
        row(w("pw", F - K - 16, F + 16), 128, p, DROP)
    for p, c in ((72, 0.0), (88, DROP), (104, 0.0), (120, DROP)):
        row(w("fid"), K, p, c)
    iota(w("num"), [[1, PLANE]], 0, 0)
    iota(w("dif"), [[0, 6], [1, 16]], 0, 0)
    iota(w("revi"), [[-16, 6]], K - 1, 0)

    def home(e, lo, hi):
        if hi <= 256:
            return w("xp%d" % e, 2 * lo + 1, 2 * hi, 2)
        return w("xp%d" % e, 4 * lo - 511, 4 * hi - 512, 4)

    def spread_u(a):
        off = w("uoff", 8 * a, 8 * a + 8)
        cp(words(w("ubc", 128 * a, 128 * a + 128)), by(words(w("qu")), off))
        act(w("sbc", 128 * a, 128 * a + 128), by(w("su"), off), ACT.Copy)

    def fired(t):
        act(w("flb"), by(w("num"), w("fo%d" % t, 0, 6)), ACT.Copy)
        act(w("flr%d" % t), by(w("flb"), w("rev")), ACT.Copy)
        dma("y", "dfl%d" % t, hbm(T.fl[t:t + 1, :]), w("flr%d" % t, 0, K, 1, 0, 1))

    def bank(b, lo=0, hi=V):
        return w("ps", 512 * b + lo, 512 * b + hi)

    for t in range(ROUNDS):
        qh, sh = "qh%d" % t, "sh%d" % t
        uq, us = w("ubc", 128 * t, 128 * t + 128), w("sbc", 128 * t, 128 * t + 128)

        def gather(q, e, lo, hi):
            out = w("hs", 4 * lo + e, 4 * hi, 4)
            if t == 0:
                src = by(w("xs"), w("o4", 48 * e + lo // 16, 48 * e + hi // 16))
                if q == "v":
                    cp(out, src)
                else:
                    act(out, src, ACT.Copy)
            else:
                src = by(w("xp%d" % e), w("fvu", lo // 16, hi // 16))
                if q == "v":
                    ts(out, src, 0.015625, None, ALU.mult)
                else:
                    act(out, src, ACT.Copy, scale=0.015625)

        def half(h):
            quant(w(qh, V * h, V * h + V), w(sh, V * h, V * h + V), w("hs", 4 * V * h, 4 * V * h + 4 * V))
            cols = [(bank(c % 3, 0, 128), w(qh, 128 * c, 128 * c + 128), w(sh, 128 * c, 128 * c + 128), uq, us)
                    for c in range(3 * h, 3 * h + 3)]
            rows = [(bank(b), uq, us, w(qh, V * h, V * h + V), w(sh, V * h, V * h + V)) for b in ((3, 4), (5,))[h]]
            for a in (rows + cols if h else cols + rows):
                mm(*a)

        def col(c):
            return w("scol", c, c + 1)

        lt, le = ALU.is_lt, ALU.is_le
        mine_v = {0: [(1, 0, 384, le)], 1: [(0, 0, 128, lt), (0, 256, 384, le), (1, 0, 384, le)],
                  2: [(1, 0, 384, le)], 3: [(1, 128, 384, le)],
                  4: [(1, 0, 128, lt), (1, 256, 384, le)],
                  5: [(0, N5, 384, lt), (1, 0, 256, lt)]}
        early = [(2, 0, 256, False), (0, 128, 384, True)]
        late = [(5, 0, N5, False), (4, 0, 384, False), (3, 0, 384, False)]
        place = {}
        at = 0
        for j in early + late:
            place[j] = at
            at += j[2] - j[1]

        def scores(h):
            act(w("scol", 3 * h, 3 * h + 3), w("ps", 0, 1536, 512), ACT.Copy)
            act(w("gap", 3 * h, 3 * h + 3), w("ps", 0, 1536, 512), ACT.Abs, bias=TINY, scale=STEP)

        def bar(c):
            out = w("bar", 128 * c, 128 * c + 128)
            if c in VB:
                ts(out, w("tri"), w("gap", c, c + 1), col(c), ALU.mult, ALU.add)
            else:
                act(out, w("tri"), ACT.Identity, bias=col(c), scale=w("gap", c, c + 1))

        def block(c):
            d = 128 * (c % 3)
            tt(w("flags", FW * c, FW * c + 128), bank(3 + 2 * (c // 3), d, d + 128), w("bar", 128 * c, 128 * c + 128), lt)

        def compare(c, which):
            a = FW * c + 128
            for i, (h, lo, hi, o) in enumerate(mine_v[c]):
                if i in which and hi > lo:
                    ts(w("flags", a, a + hi - lo), bank(3 + 2 * h, lo, hi), col(c), None, o)
                a += hi - lo

        def count(c):
            n = (128 + sum(j[2] - j[1] for j in mine_v[c])) // 2
            init = w("acc", c, c + 1) if any(j[0] == c for j in early + late) else 0.0
            scan(w("cnt", 6 * (CW - n) + c, 6 * CW, 6), w("flags", FW * c, FW * c + n),
                 w("flags", FW * c + n, FW * c + 2 * n), init, ALU.add, ALU.add)

        def sign1(j):
            act(w("sg", place[j], place[j] + j[2] - j[1]), bank(4, j[1], j[2]), ACT.Sign, bias=col(j[0]), scale=-1.0)

        def sign2(j):
            a = w("sg", place[j], place[j] + j[2] - j[1])
            if j[3]:
                act(a, a, ACT.Sign, bias=1.0, accum=w("acc", j[0], j[0] + 1))
            else:
                act(a, a, ACT.Relu, accum=w("acc", j[0], j[0] + 1))

        if t == 0:
            gather("s", 1, 0, V)
            gather("v", 0, 0, V)
            gather("s", 3, 0, V)
            quant(w("qu"), w("su"), w("ub"))
            gather("v", 2, 0, V)
            spread_u(0)
        else:
            gather("s", 0, 0, V)
            gather("s", 1, 0, V)
            gather("v", 2, 0, V)
            gather("s", 3, 0, V)
            gather("v", 3, V, V + GA)
        gather("s", 0, V, F)
        gather("s", 1, V, F)
        half(0)
        gather("v", 2, V, F)
        scores(0)
        gather("v", 3, V + GA if t else V, F)
        for c in range(3):
            bar(c)
        compare(1, [0])
        half(1)
        compare(1, [1])
        sign1(early[0])
        sign1(early[1])
        sign2(early[0])
        sign2(early[1])
        for c in range(3):
            block(c)
        scores(1)
        sign1(late[0])
        for c in range(3, 6):
            if c not in VB:
                bar(c)
        sign1(late[1])
        sign2(late[0])
        sign1(late[2])
        sign2(late[1])
        sign2(late[2])
        compare(1, [2])
        compare(0, [0])
        count(1)
        compare(2, [0])
        for c in range(3, 6):
            if c in VB:
                bar(c)
        count(0)
        compare(5, [0, 1])
        count(2)
        for c in (5, 4, 3):
            block(c)
        compare(4, [0, 1])
        compare(3, [0])
        count(5)
        count(4)
        count(3)
        fo = w("fo%d" % t, 0, 6)
        if t == 0:
            act(w("fvrow"), by(w("num"), w("fvu")), ACT.Identity, bias=-1.0)
        else:
            fired(t - 1)
        cp(by(w("pw"), w("cnt", 6 * CW - 6, 6 * CW)), w("fid"))
        turn(w("tr", 0, 128), w("pw", F - K - 16, F + 16))
        turn(w("tr", 128, 224), w("pw", F - K, F))
        scan(w("u2", 0, 28, 1, 0, 64), w("tr", 0, 224, 8, 0, 64), w("tr", 0, 224, 8, 64, 128), 0.0, ALU.max, ALU.add)
        for a in (0, 32, 64, 96):
            tt(w("u3", 0, 7, 1, a, a + 32), w("u2", 2, 28, 4, 0, 32), w("u2", 2, 28, 4, 32, 64), ALU.add)
        cp(w("fo%d" % t), by(w("u3"), w("turn", 0, 1)))
        remote(t, "list%d" % t, w("lst%d" % t), fo, mine[t][0])
        cp(words(w("slotq%d" % t)), by(words(w(qh)), fo))
        act(w("slots%d" % t), by(w(sh), fo), ACT.Copy)
        remote(t, "data%d" % t, octets(w("landq%d" % t, 0, K)), octets(w("slotq%d" % t)), mine[t][1])
        remote(t, "data%d" % t, w("lands%d" % t, 0, K), w("slots%d" % t), mine[t][0])
        if t == 0:
            ts(w("msk"), w("dif"), place_, None, ALU.is_equal)
            ts(w("rev"), w("revi"), place_, None, ALU.subtract)
            ts(w("cc"), w("num", 0, SEG), own_, 2048.0, ALU.is_le, ALU.mult)
        quant(w("landq%d" % t, K, K + 128), w("lands%d" % t, K, K + 128), w("xs", 0, 512))
        if t == 0:
            for e in range(4):
                for lo, hi in SPANS:
                    ts(home(e, lo, hi), w("xs", 4 * lo + e, 4 * hi, 4), 64.0, None, ALU.mult)
        if t < ROUNDS - 1:
            spread_u(t + 1)
            ts(w("pw", F - K, F), w("num", 0, K), 0.0, w("pw", F + 15, F + 16), ALU.mult, ALU.add)
        if t == 1:
            quant(w("qwy"), w("swy"), w("wyb"))
        if t == ROUNDS - 1:
            fired(t)
        lst = w("lst%d" % t)

        def old(e):
            for x in (e, e + 1):
                ts(w("f4", 6 * x, 6 * x + 6), lst, 4.0, float(x), ALU.mult, ALU.add)
            act(w("x32", K * e, K * e + 2 * K), by(w("hs"), w("f4", 6 * e, 6 * e + 12)), ACT.Copy, scale=32.0)

        def blend(b):
            tt(w("zb", K * b, K * b + K), bank(b, 0, K), w("x32", K * b, K * b + K), ALU.add)

        tt(w("gt"), by(w("fvrow"), lst), w("msk"), ALU.mult)
        act(w("gu", 0, K), by(w("fvrow"), lst), ACT.Copy)
        old(0)
        scan(w("s1"), w("rst"), w("gt"), 0.0, ALU.mult, ALU.add)
        old(2)
        for m in range(6):
            v = w("s1", 16 * m + 15, 16 * m + 16)
            ts(w("ne", SEG * m, SEG * m + SEG - 16 * m), w("gu", 16 * m, SEG), v, v, ALU.not_equal, ALU.add)
        for m in range(6):
            n = SEG - 16 * m
            scan(w("win", 96 * m + m, 6 * SEG, 6), w("cc", 0, n), w("ne", SEG * m, SEG * m + n), 0.0, ALU.max, ALU.min)
        for b in range(4):
            mm(bank(b, 0, 128), w("qw", 128 * b, 128 * b + 128), w("sw", 128 * b, 128 * b + 128),
               w("landq%d" % t, 0, 128), w("lands%d" % t, 0, 128))
        blend(0)
        blend(1)
        for b in range(4):
            cp(by(w("xp%d" % b), w("win", 6 * SEG - 6, 6 * SEG)), w("zb", K * b, K * b + K))
            if b < 2:
                blend(b + 2)

    for e in range(3):
        for lo, hi in SPANS:
            act(w("xs", 4 * lo + e, 4 * hi, 4), home(e, lo, hi), ACT.Copy, scale=0.015625)
    for lo, hi in SPANS:
        ts(w("xs", 4 * lo + 3, 4 * hi, 4), home(3, lo, hi), 0.015625, None, ALU.mult)
    for i, lo in enumerate((256, 0, 128)):
        hi = lo + 128
        quant(w("qx", lo, hi), w("sx", lo, hi), w("xs", 4 * lo, 4 * hi))
        mm(bank(4 + i, 0, 128), w("qwy"), w("swy"), w("qx", lo, hi), w("sx", lo, hi))
        if i == 0:
            dma("y", "dout", hbm(T.oc[:, 4 * lo:4 * hi]), octets(w("qx", lo, hi)))
    dma("y", "dout", hbm(T.oc[:, 0:1024]), octets(w("qx", 0, 256)))
    act(w("ysb", 256, 384), bank(4, 0, 128), ACT.Copy)
    cp(w("ysb", 0, 128), bank(5, 0, 128))
    cp(w("ysb", 128, 256), bank(6, 0, 128))
    dma("s", "dy", hbm(T.y[:]), w("ysb"))
    for k in range(4):
        dma("y", "dout", hbm(T.osc[4 * k:4 * k + 4, :]), w("sx", 0, V, 1, 32 * k, 32 * k + 4))
    tail = ["cp", "cs", "cv", "dout", "dy"]
    for sem in [s for s in SEMAPHORES if s not in tail] + tail:
        if total.get(sem, 0):
            g.wait_ge(T.sem[sem], total[sem])
